import numpy as np
import ml_dtypes


def mxq(x, axis, fmt="e4m3"):
    dtype, down = {"e4m3": (ml_dtypes.float8_e4m3fn, 7), "e5m2": (ml_dtypes.float8_e5m2, 14)}[fmt]
    v = np.moveaxis(np.asarray(x, np.float32).astype(ml_dtypes.bfloat16).astype(np.float64), axis, -1)
    blocks = v.reshape(v.shape[:-1] + (-1, 32))
    amax = np.abs(blocks).max(-1, keepdims=True)
    byte = np.maximum(np.where(amax > 0, np.frexp(amax)[1] - 1 + 127, 0) - down, 1)
    scale = np.exp2(byte - 127.0)
    codes = (blocks / scale).astype(np.float32).astype(dtype).astype(np.float64)
    return np.moveaxis((codes * scale).reshape(v.shape), -1, axis)


WIDE = False


def mx_kscale(k):
    if not WIDE:
        return np.ones(k)
    levels = np.array([10, -10, 5, -5, 0])
    if k % 512:
        return np.exp2(np.random.permutation(np.resize(levels, k // 32))).repeat(32)
    a = np.empty((k // 512, 16))
    for p in range(k // 512):
        a[p, :8] = np.random.permutation(np.resize(levels, 8))
        for g in range(8):
            far = levels[np.abs(levels - a[p, g]) >= 10]
            a[p, g + 8] = far[np.random.randint(len(far))]
    return np.exp2(a.ravel()).repeat(32)


def f64(x):
    return np.asarray(x).astype(np.float64)


def striped8(idx):
    return np.concatenate([x.reshape(-1, 16).T for x in idx]).astype(np.uint16)


def runs(offs, k):
    lists = np.stack([offs[16 * r : 16 * r + 16].T.reshape(-1) for r in range(8)]).astype(np.int64)
    return lists[np.arange(k) % 512 // 64]


def pack_weight(w):
    k, n = w.shape
    w = f64(np.asarray(w, np.float32).astype(ml_dtypes.bfloat16)).reshape(k // 32, 32, n)
    amax = np.abs(w).max(1)
    byte = np.clip(np.where(amax > 0, np.frexp(amax)[1] - 1 + 127 - 7, 1), 1, 254)
    scaled = (w * np.exp2(127.0 - byte)[:, None, :]).reshape(k, n).astype(np.float32)
    words = np.ascontiguousarray(scaled.reshape(k // 512, 128, 4, n).transpose(0, 1, 3, 2)).astype(ml_dtypes.float8_e4m3fn).view(np.uint8)
    return words, np.ascontiguousarray(byte.astype(np.uint8).reshape(k // 512, 16, n))


def unpack_weight(words, scales):
    g, p, n, _ = words.shape
    vals = np.ascontiguousarray(words).view(ml_dtypes.float8_e4m3fn).astype(np.float64) * np.repeat(np.exp2(scales.astype(np.float64) - 127.0), 8, axis=1)[..., None]
    return vals.transpose(0, 1, 3, 2).reshape(g * 512, n)


def relu(v):
    return np.maximum(v, 0.0)


K, T, S, V, N, H = 512, 2048, 1024, 512, 512, 512


def setup_inputs():
    n = np.random.standard_normal
    s = mx_kscale(K)[:, None]
    u = mx_kscale(H)
    packed_xT = pack_weight(n((K, T)) * s)
    return {
        "x_words": packed_xT[0],
        "x_scales": packed_xT[1],
        "w1": (n((K, H)) / np.sqrt(K) / s * u).astype(np.float32),
        "w2": (n((H, N)) / np.sqrt(2 * H) / u[:, None]).astype(np.float32),
        "w3": (n((H, N)) / np.sqrt(2 * H) / u[:, None]).astype(np.float32),
        "offs": striped8(np.stack([np.random.permutation(T)[:S] for _ in range(8)])),
        "order": striped8(np.stack([np.random.permutation(S) for _ in range(8)])),
    }


def reference(x_words, x_scales, w1, w2, w3, offs, order):
    xq = unpack_weight(x_words, x_scales)[np.arange(K)[:, None], runs(offs, K)]
    y = mxq(f64(w1), 0, "e4m3").T @ xq
    o = y[np.arange(H)[:, None], runs(order, H)]
    mx = o.reshape(H, V, 2).max(axis=2)
    z = relu(mx)
    mn = o.reshape(H, V, 2).min(axis=2)
    z2 = relu(mn)
    return mxq(f64(w2), 0, "e4m3").T @ mxq(z, 0, "e4m3") + mxq(f64(w3), 0, "e4m3").T @ mxq(z2, 0, "e4m3")

@@ -1,0 +1,187 @@
+from contextlib import ExitStack
+
+import concourse.mybir as mybir
+
+K, T, S, V, N, H = 512, 2048, 1024, 512, 512, 512
+FLOPS = 2 * K * H * S + 2 * 2 * H * N * V
+
+F32 = mybir.dt.float32
+BF16 = mybir.dt.bfloat16
+I32 = mybir.dt.int32
+U32 = mybir.dt.uint32
+U16 = mybir.dt.uint16
+U8 = mybir.dt.uint8
+FP8X4 = mybir.dt.float8_e4m3fn_x4
+RELU = mybir.ActivationFunctionType.Relu
+MAX = mybir.AluOpType.max
+MIN = mybir.AluOpType.min
+
+P = 128
+PACK = 4
+BANK = 512
+CHUNKS = (256,128,128)
+WOVEN_BY_SCALAR = ()
+
+
+def tile_picked_winmax_relu_p_kernel(tc, x_words, x_scales, w1, w2, w3, offs, order, out):
+    nc = tc.nc
+    with ExitStack() as ctx:
+        keep = ctx.enter_context(tc.tile_pool(name="keep", bufs=1))
+        psum = ctx.enter_context(tc.psum_pool(name="psum", bufs=1))
+
+        offs_sb = keep.tile([P, S // 16], U16, name="offs_sb")
+        order_sb = keep.tile([P, S // 16], U16, name="order_sb")
+        scale_table = keep.tile([P, T], U8, name="scale_table", align_bytes=64)
+        word_table = keep.tile([P, T], U32, name="word_table", align_bytes=64)
+        w1_raw = [keep.tile([P, PACK, H // 2], F32, name="w1_raw%d" % h, align_bytes=64) for h in range(2)]
+
+        nc.sync.dma_start(offs_sb[:], offs)
+        nc.sync.dma_start(
+            scale_table[:].bitcast(I32),
+            x_scales[0].bitcast(I32).unsqueeze(1).to_broadcast([16, 8, T // 4]),
+        )
+        nc.sync.dma_start(word_table[:].bitcast(I32), x_words[0].rearrange("p c r -> p (c r)").bitcast(I32))
+        w1_rows = w1.rearrange("(p j) c -> p j c", j=PACK)
+        for h in range(2):
+            nc.sync.dma_start(w1_raw[h][:], w1_rows[:, :, h * (H // 2) : (h + 1) * (H // 2)])
+        nc.sync.dma_start(order_sb[:], order)
+
+        x_plane = keep.tile([P, S], U8, name="x_plane", align_bytes=64)
+        nc.vector.memset(x_plane[:].bitcast(I32), 0)
+        picked_scales = keep.tile([P, S], U8, name="picked_scales", tag="late", align_bytes=64)
+        nc.vector.tensor_copy(picked_scales[:], scale_table[:].indirect(offs_sb[:]))
+        for q in range(4):
+            nc.scalar.dma_start(
+                x_plane[32 * q : 32 * q + 4, :].bitcast(I32),
+                picked_scales[32 * q : 32 * q + 32 : 8, :].bitcast(I32),
+            )
+        w_raw = keep.tile([P, 2, PACK, N], F32, name="w_raw", tag="late", align_bytes=64)
+        for u, w in enumerate((w2, w3)):
+            nc.sync.dma_start(w_raw[:, u], w.rearrange("(p j) c -> p j c", j=PACK))
+        x_codes = keep.tile([P, S], U32, name="x_codes", align_bytes=64)
+        nc.vector.tensor_copy(x_codes[:], word_table[:].indirect(offs_sb[:]))
+
+        w1_bf = keep.tile([P, PACK, P, PACK], BF16, name="w1_bf", align_bytes=64)
+        for h, cast in enumerate((nc.scalar.copy, nc.vector.tensor_copy)):
+            cast(
+                w1_bf[:, :, h * (P // 2) : (h + 1) * (P // 2), :].rearrange("p t m j -> p m j t"),
+                w1_raw[h][:].rearrange("p j (m t) -> p m j t", t=PACK),
+            )
+        w1_codes = keep.tile([P, H], U32, name="w1_codes", align_bytes=64)
+        w1_plane = keep.tile([P, H], U8, name="w1_plane", align_bytes=64)
+        y = [keep.tile([P, S], F32, name="y%d" % t, align_bytes=64) for t in range(PACK)]
+        for t in range(PACK):
+            cols = slice(t * P, (t + 1) * P)
+            nc.vector.quantize_mx(
+                out=w1_codes[:, cols].bitcast(FP8X4),
+                scales=w1_plane[:, cols],
+                in_=w1_bf[:, t, :, :].rearrange("p m j -> p (m j)"),
+            )
+        for t in range(PACK):
+            cols = slice(t * P, (t + 1) * P)
+            for h in range(S // BANK):
+                places = slice(h * BANK, (h + 1) * BANK)
+                acc = psum.tile([P, BANK], F32, name="acc", tag="bank%d" % (2 * t + h))
+                nc.tensor.matmul_mx(
+                    out=acc[:],
+                    lhsT=w1_codes[:, cols].bitcast(FP8X4),
+                    lhsT_scale=w1_plane[:, cols],
+                    rhs=x_codes[:, places].bitcast(FP8X4),
+                    rhs_scale=x_plane[:, places],
+                    start=True,
+                    stop=True,
+                )
+                nc.scalar.activation(y[t][:, places], acc[:], RELU)
+
+        w_codes = [keep.tile([P, N], U32, name="w_codes%d" % u, align_bytes=64) for u in range(2)]
+        w_plane = [keep.tile([P, N], U8, name="w_plane%d" % u, align_bytes=64) for u in range(2)]
+        w_bf = [keep.tile([P, N * PACK], BF16, name="w_bf%d" % u, align_bytes=64) for u in range(2)]
+
+        def cast_weights(u):
+            nc.scalar.copy(
+                w_bf[u][:].rearrange("p (c i j) -> p c j i", i=4, j=PACK),
+                w_raw[:, u].rearrange("p j (c i) -> p c j i", i=4),
+            )
+
+        def quantize_weights(u):
+            nc.vector.quantize_mx(out=w_codes[u][:].bitcast(FP8X4), scales=w_plane[u][:], in_=w_bf[u][:])
+
+        out_rows = out.rearrange("(m p) v -> p m v", p=P)
+        starts = [sum(CHUNKS[:c]) for c in range(len(CHUNKS))]
+        looked_up, woven, z_bf, z_codes, z_plane = {}, {}, {}, {}, {}
+
+        def gather(c):
+            n = 2 * CHUNKS[c]
+            looked_up[c] = keep.tile([P, PACK, n], BF16, name="looked_up%d" % c, align_bytes=64)
+            entries = order_sb[:, starts[c] // 8 : (starts[c] + CHUNKS[c]) // 8]
+            for t in range(PACK):
+                nc.vector.tensor_copy(looked_up[c][:, t, :], y[t][:].indirect(entries))
+
+        def weave(c):
+            n = 2 * CHUNKS[c]
+            woven[c] = keep.tile([P, n * PACK], BF16, name="woven%d" % c, align_bytes=64)
+            nc.scalar.copy(
+                woven[c][:].rearrange("p (c i t) -> p c t i", i=4, t=PACK),
+                looked_up[c][:].rearrange("p t (c i) -> p c t i", i=4),
+            )
+
+        def pool_pairs(c, u):
+            z_bf[c, u] = keep.tile([P, CHUNKS[c] * PACK], BF16, name="z_bf%d_%d" % (c, u), align_bytes=64)
+            if c in woven:
+                pairs = woven[c][:].rearrange("p (v s t) -> p s v t", s=2, t=PACK)
+                dst = z_bf[c, u][:].rearrange("p (v t) -> p v t", t=PACK)
+            else:
+                pairs = looked_up[c][:].rearrange("p t (c i s) -> p s c t i", i=4, s=2)
+                dst = z_bf[c, u][:].rearrange("p (c i t) -> p c t i", i=4, t=PACK)
+            nc.vector.tensor_tensor(dst, pairs[:, 0], pairs[:, 1], (MAX, MIN)[u])
+
+        def quantize_pooled(c, u):
+            z_codes[c, u] = keep.tile([P, CHUNKS[c]], U32, name="z_codes%d_%d" % (c, u), align_bytes=64)
+            z_plane[c, u] = keep.tile([P, CHUNKS[c]], U8, name="z_plane%d_%d" % (c, u), align_bytes=64)
+            nc.vector.quantize_mx(out=z_codes[c, u][:].bitcast(FP8X4), scales=z_plane[c, u][:], in_=z_bf[c, u][:])
+
+        def project(c):
+            last = c == len(CHUNKS) - 1
+            banks = [psum.tile([P, CHUNKS[c]], F32, name="res", tag="bank%d" % (4 * (c % 2) + m)) for m in range(N // P)]
+            for u in range(2):
+                for m in range(N // P):
+                    cols = slice(m * P, (m + 1) * P)
+                    nc.tensor.matmul_mx(
+                        out=banks[m][:],
+                        lhsT=w_codes[u][:, cols].bitcast(FP8X4),
+                        lhsT_scale=w_plane[u][:, cols],
+                        rhs=z_codes[c, u][:].bitcast(FP8X4),
+                        rhs_scale=z_plane[c, u][:],
+                        start=(u == 0),
+                        stop=(u == 1),
+                    )
+            for half in range(2):
+                staged = keep.tile([P, 2, CHUNKS[c]], F32, name="staged%d_%d" % (c, half), align_bytes=64)
+                for r in range(2):
+                    m = 2 * r + half
+                    leave = nc.vector.tensor_copy if last and half == 1 else nc.scalar.copy
+                    leave(staged[:, r, :], banks[m][:])
+                nc.sync.dma_start(out_rows[:, half::2, starts[c] : starts[c] + CHUNKS[c]], staged[:])
+
+        cast_weights(0)
+        cast_weights(1)
+        gather(0)
+        pool_pairs(0, 0)
+        pool_pairs(0, 1)
+        gather(1)
+        quantize_weights(0)
+        quantize_weights(1)
+        quantize_pooled(0, 0)
+        quantize_pooled(0, 1)
+        project(0)
+        pool_pairs(1, 0)
+        pool_pairs(1, 1)
+        gather(2)
+        quantize_pooled(1, 0)
+        quantize_pooled(1, 1)
+        project(1)
+        pool_pairs(2, 0)
+        pool_pairs(2, 1)
+        quantize_pooled(2, 0)
+        quantize_pooled(2, 1)
+        project(2)

@@ -20,7 +20,7 @@ P = 128
 PACK = 4
 BANK = 512
 CHUNKS = (256,128,128)
-WOVEN_BY_SCALAR = ()
+WOVEN_BY_SCALAR = (0, 1)
 
 
 def tile_picked_winmax_relu_p_kernel(tc, x_words, x_scales, w1, w2, w3, offs, order, out):
@@ -31,7 +31,7 @@ def tile_picked_winmax_relu_p_kernel(tc, x_words, x_scales, w1, w2, w3, offs, or
 
         offs_sb = keep.tile([P, S // 16], U16, name="offs_sb")
         order_sb = keep.tile([P, S // 16], U16, name="order_sb")
-        scale_table = keep.tile([P, T], U8, name="scale_table", align_bytes=64)
+        scale_table = keep.tile([P, T], U8, name="scale_table", tag="late", align_bytes=64)
         word_table = keep.tile([P, T], U32, name="word_table", align_bytes=64)
         w1_raw = [keep.tile([P, PACK, H // 2], F32, name="w1_raw%d" % h, align_bytes=64) for h in range(2)]
 
@@ -46,28 +46,38 @@ def tile_picked_winmax_relu_p_kernel(tc, x_words, x_scales, w1, w2, w3, offs, or
             nc.sync.dma_start(w1_raw[h][:], w1_rows[:, :, h * (H // 2) : (h + 1) * (H // 2)])
         nc.sync.dma_start(order_sb[:], order)
 
+        warm_in = keep.tile([P, 1], F32, name="warm_in")
+        warm_out = keep.tile([P, 1], F32, name="warm_out")
+        nc.gpsimd.memset(warm_in[:], 0.0)
+        nc.scalar.activation(warm_out[:], warm_in[:], RELU)
         x_plane = keep.tile([P, S], U8, name="x_plane", align_bytes=64)
         nc.vector.memset(x_plane[:].bitcast(I32), 0)
-        picked_scales = keep.tile([P, S], U8, name="picked_scales", tag="late", align_bytes=64)
+        picked_scales = keep.tile([P, S], U8, name="picked_scales", align_bytes=64)
         nc.vector.tensor_copy(picked_scales[:], scale_table[:].indirect(offs_sb[:]))
         for q in range(4):
-            nc.scalar.dma_start(
+            nc.sync.dma_start(
                 x_plane[32 * q : 32 * q + 4, :].bitcast(I32),
                 picked_scales[32 * q : 32 * q + 32 : 8, :].bitcast(I32),
             )
-        w_raw = keep.tile([P, 2, PACK, N], F32, name="w_raw", tag="late", align_bytes=64)
-        for u, w in enumerate((w2, w3)):
-            nc.sync.dma_start(w_raw[:, u], w.rearrange("(p j) c -> p j c", j=PACK))
-        x_codes = keep.tile([P, S], U32, name="x_codes", align_bytes=64)
+        w_raw = keep.tile([P, 2 * PACK * N], F32, name="w_raw", tag="late", align_bytes=64)
+        pieces = ((0, 0, N // 2), (0, N // 2, N), (1, 0, N))
+        w_rows = [w.rearrange("(p j) c -> p j c", j=PACK) for w in (w2, w3)]
+
+        def raw_piece(u, c0, c1):
+            return w_raw[:, PACK * (u * N + c0) : PACK * (u * N + c1)].rearrange("p (j c) -> p j c", j=PACK)
+
+        for u, c0, c1 in pieces:
+            nc.sync.dma_start(raw_piece(u, c0, c1), w_rows[u][:, :, c0:c1])
+        x_codes = keep.tile([P, S], U32, name="x_codes", tag="x_codes", align_bytes=64)
         nc.vector.tensor_copy(x_codes[:], word_table[:].indirect(offs_sb[:]))
 
         w1_bf = keep.tile([P, PACK, P, PACK], BF16, name="w1_bf", align_bytes=64)
-        for h, cast in enumerate((nc.scalar.copy, nc.vector.tensor_copy)):
+        for cast, h, m0, m1 in ((nc.scalar.copy, 0, 0, 64), (nc.scalar.copy, 1, 0, 24), (nc.vector.tensor_copy, 1, 24, 64)):
             cast(
-                w1_bf[:, :, h * (P // 2) : (h + 1) * (P // 2), :].rearrange("p t m j -> p m j t"),
-                w1_raw[h][:].rearrange("p j (m t) -> p m j t", t=PACK),
+                w1_bf[:, :, h * (P // 2) + m0 : h * (P // 2) + m1, :].rearrange("p t m j -> p m j t"),
+                w1_raw[h][:].rearrange("p j (m t) -> p m j t", t=PACK)[:, m0:m1],
             )
-        w1_codes = keep.tile([P, H], U32, name="w1_codes", align_bytes=64)
+        w1_codes = keep.tile([P, H], U32, name="w1_codes", tag="w1_codes", align_bytes=64)
         w1_plane = keep.tile([P, H], U8, name="w1_plane", align_bytes=64)
         y = [keep.tile([P, S], F32, name="y%d" % t, align_bytes=64) for t in range(PACK)]
         for t in range(PACK):
@@ -93,18 +103,23 @@ def tile_picked_winmax_relu_p_kernel(tc, x_words, x_scales, w1, w2, w3, offs, or
                 )
                 nc.scalar.activation(y[t][:, places], acc[:], RELU)
 
-        w_codes = [keep.tile([P, N], U32, name="w_codes%d" % u, align_bytes=64) for u in range(2)]
+        w_codes = [keep.tile([P, N], U32, name="w_codes%d" % u, align_bytes=64) for u in range(1)]
         w_plane = [keep.tile([P, N], U8, name="w_plane%d" % u, align_bytes=64) for u in range(2)]
-        w_bf = [keep.tile([P, N * PACK], BF16, name="w_bf%d" % u, align_bytes=64) for u in range(2)]
+        w_bf = {}
 
-        def cast_weights(u):
-            nc.scalar.copy(
-                w_bf[u][:].rearrange("p (c i j) -> p c j i", i=4, j=PACK),
-                w_raw[:, u].rearrange("p j (c i) -> p c j i", i=4),
+        def cast_weights(cast, tag, u, c0, c1):
+            w_bf[u, c0] = keep.tile([P, (c1 - c0) * PACK], BF16, name="w_bf%d_%d" % (u, c0), tag=tag, align_bytes=64)
+            cast(
+                w_bf[u, c0][:].rearrange("p (c i j) -> p c j i", i=4, j=PACK),
+                raw_piece(u, c0, c1).rearrange("p j (c i) -> p c j i", i=4),
             )
 
-        def quantize_weights(u):
-            nc.vector.quantize_mx(out=w_codes[u][:].bitcast(FP8X4), scales=w_plane[u][:], in_=w_bf[u][:])
+        def quantize_weights(u, c0, c1):
+            if u == 1:
+                w_codes.append(keep.tile([P, N], U32, name="w_codes1", tag="z_bf0", align_bytes=64))
+            nc.vector.quantize_mx(
+                out=w_codes[u][:, c0:c1].bitcast(FP8X4), scales=w_plane[u][:, c0:c1], in_=w_bf[u, c0][:]
+            )
 
         out_rows = out.rearrange("(m p) v -> p m v", p=P)
         starts = [sum(CHUNKS[:c]) for c in range(len(CHUNKS))]
@@ -112,33 +127,43 @@ def tile_picked_winmax_relu_p_kernel(tc, x_words, x_scales, w1, w2, w3, offs, or
 
         def gather(c):
             n = 2 * CHUNKS[c]
-            looked_up[c] = keep.tile([P, PACK, n], BF16, name="looked_up%d" % c, align_bytes=64)
+            looked_up[c] = keep.tile([P, PACK, n], BF16, name="looked_up%d" % c, tag=("looked_up0", "w1_codes", "looked_up0")[c], align_bytes=64)
             entries = order_sb[:, starts[c] // 8 : (starts[c] + CHUNKS[c]) // 8]
             for t in range(PACK):
                 nc.vector.tensor_copy(looked_up[c][:, t, :], y[t][:].indirect(entries))
 
         def weave(c):
             n = 2 * CHUNKS[c]
-            woven[c] = keep.tile([P, n * PACK], BF16, name="woven%d" % c, align_bytes=64)
+            woven[c] = keep.tile([P, n * PACK], BF16, name="woven%d" % c, tag="late" if c == 1 else "woven%d" % c, align_bytes=64)
             nc.scalar.copy(
                 woven[c][:].rearrange("p (c i t) -> p c t i", i=4, t=PACK),
                 looked_up[c][:].rearrange("p t (c i) -> p c t i", i=4),
             )
 
-        def pool_pairs(c, u):
-            z_bf[c, u] = keep.tile([P, CHUNKS[c] * PACK], BF16, name="z_bf%d_%d" % (c, u), align_bytes=64)
-            if c in woven:
-                pairs = woven[c][:].rearrange("p (v s t) -> p s v t", s=2, t=PACK)
-                dst = z_bf[c, u][:].rearrange("p (v t) -> p v t", t=PACK)
-            else:
-                pairs = looked_up[c][:].rearrange("p t (c i s) -> p s c t i", i=4, s=2)
-                dst = z_bf[c, u][:].rearrange("p (c i t) -> p c t i", i=4, t=PACK)
-            nc.vector.tensor_tensor(dst, pairs[:, 0], pairs[:, 1], (MAX, MIN)[u])
+        def pool_pairs(c):
+            width = CHUNKS[c] * PACK
+            z_bf[c] = keep.tile([P, 2 * width], BF16, name="z_bf%d" % c, tag="late" if c == 2 else "z_bf%d" % c, align_bytes=64)
+            for u, op in enumerate((MAX, MIN)):
+                pooled = z_bf[c][:, u * width : (u + 1) * width]
+                if c in woven:
+                    pairs = woven[c][:].rearrange("p (v s t) -> p s v t", s=2, t=PACK)
+                    dst = pooled.rearrange("p (v t) -> p v t", t=PACK)
+                else:
+                    pairs = looked_up[c][:].rearrange("p t (c i s) -> p s c t i", i=4, s=2)
+                    dst = pooled.rearrange("p (c i t) -> p c t i", i=4, t=PACK)
+                nc.vector.tensor_tensor(dst, pairs[:, 0], pairs[:, 1], op)
 
-        def quantize_pooled(c, u):
-            z_codes[c, u] = keep.tile([P, CHUNKS[c]], U32, name="z_codes%d_%d" % (c, u), align_bytes=64)
-            z_plane[c, u] = keep.tile([P, CHUNKS[c]], U8, name="z_plane%d_%d" % (c, u), align_bytes=64)
-            nc.vector.quantize_mx(out=z_codes[c, u][:].bitcast(FP8X4), scales=z_plane[c, u][:], in_=z_bf[c, u][:])
+        def quantize_pooled(c, calls):
+            z_codes[c] = keep.tile([P, 2 * CHUNKS[c]], U32, name="z_codes%d" % c, align_bytes=64)
+            z_plane[c] = keep.tile([P, 2 * CHUNKS[c]], U8, name="z_plane%d" % c, align_bytes=64)
+            words = 2 * CHUNKS[c] // calls
+            for i in range(calls):
+                cols = slice(i * words, (i + 1) * words)
+                nc.vector.quantize_mx(
+                    out=z_codes[c][:, cols].bitcast(FP8X4),
+                    scales=z_plane[c][:, cols],
+                    in_=z_bf[c][:, PACK * i * words : PACK * (i + 1) * words],
+                )
 
         def project(c):
             last = c == len(CHUNKS) - 1
@@ -150,8 +175,8 @@ def tile_picked_winmax_relu_p_kernel(tc, x_words, x_scales, w1, w2, w3, offs, or
                         out=banks[m][:],
                         lhsT=w_codes[u][:, cols].bitcast(FP8X4),
                         lhsT_scale=w_plane[u][:, cols],
-                        rhs=z_codes[c, u][:].bitcast(FP8X4),
-                        rhs_scale=z_plane[c, u][:],
+                        rhs=z_codes[c][:, u * CHUNKS[c] : (u + 1) * CHUNKS[c]].bitcast(FP8X4),
+                        rhs_scale=z_plane[c][:, u * CHUNKS[c] : (u + 1) * CHUNKS[c]],
                         start=(u == 0),
                         stop=(u == 1),
                     )
@@ -163,25 +188,23 @@ def tile_picked_winmax_relu_p_kernel(tc, x_words, x_scales, w1, w2, w3, offs, or
                     leave(staged[:, r, :], banks[m][:])
                 nc.sync.dma_start(out_rows[:, half::2, starts[c] : starts[c] + CHUNKS[c]], staged[:])
 
-        cast_weights(0)
-        cast_weights(1)
+        cast_weights(nc.vector.tensor_copy, "looked_up0", *pieces[0])
+        quantize_weights(*pieces[0])
+        cast_weights(nc.scalar.copy, "w1_codes", *pieces[1])
         gather(0)
-        pool_pairs(0, 0)
-        pool_pairs(0, 1)
+        weave(0)
+        cast_weights(nc.scalar.copy, "looked_up0", *pieces[2])
+        quantize_weights(*pieces[1])
         gather(1)
-        quantize_weights(0)
-        quantize_weights(1)
-        quantize_pooled(0, 0)
+        weave(1)
+        pool_pairs(0)
         quantize_pooled(0, 1)
+        quantize_weights(*pieces[2])
         project(0)
-        pool_pairs(1, 0)
-        pool_pairs(1, 1)
         gather(2)
-        quantize_pooled(1, 0)
+        pool_pairs(1)
         quantize_pooled(1, 1)
         project(1)
-        pool_pairs(2, 0)
-        pool_pairs(2, 1)
-        quantize_pooled(2, 0)
-        quantize_pooled(2, 1)
+        pool_pairs(2)
+        quantize_pooled(2, 2)
         project(2)

@@ -79,82 +79,85 @@ def tile_picked_winmax_relu_p_kernel(tc, x_words, x_scales, w1, w2, w3, offs, or
             )
         w1_codes = keep.tile([P, H], U32, name="w1_codes", tag="w1_codes", align_bytes=64)
         w1_plane = keep.tile([P, H], U8, name="w1_plane", align_bytes=64)
-        y = [keep.tile([P, S], F32, name="y%d" % t, align_bytes=64) for t in range(PACK)]
-        for t in range(PACK):
-            cols = slice(t * P, (t + 1) * P)
+        y = [keep.tile([P, S], F32, name="y%d" % t, tag="y%d" % t, align_bytes=64) for t in range(PACK)]
+        for t0, t1 in ((0, 1), (1, 2), (2, 4)):
+            cols = slice(t0 * P, t1 * P)
             nc.vector.quantize_mx(
                 out=w1_codes[:, cols].bitcast(FP8X4),
                 scales=w1_plane[:, cols],
-                in_=w1_bf[:, t, :, :].rearrange("p m j -> p (m j)"),
+                in_=w1_bf[:, t0:t1, :, :].rearrange("p t m j -> p (t m j)"),
             )
-        for t in range(PACK):
+        passes = [(t, s0, width) for t, width in enumerate((256, 512, 512, 512)) for s0 in range(0, S, width)]
+        for i, (t, s0, width) in enumerate(passes):
             cols = slice(t * P, (t + 1) * P)
-            for h in range(S // BANK):
-                places = slice(h * BANK, (h + 1) * BANK)
-                acc = psum.tile([P, BANK], F32, name="acc", tag="bank%d" % (2 * t + h))
-                nc.tensor.matmul_mx(
-                    out=acc[:],
-                    lhsT=w1_codes[:, cols].bitcast(FP8X4),
-                    lhsT_scale=w1_plane[:, cols],
-                    rhs=x_codes[:, places].bitcast(FP8X4),
-                    rhs_scale=x_plane[:, places],
-                    start=True,
-                    stop=True,
-                )
-                nc.scalar.activation(y[t][:, places], acc[:], RELU)
+            places = slice(s0, s0 + width)
+            acc = psum.tile([P, width], F32, name="acc", tag="bank%d" % (i % 8))
+            nc.tensor.matmul_mx(
+                out=acc[:],
+                lhsT=w1_codes[:, cols].bitcast(FP8X4),
+                lhsT_scale=w1_plane[:, cols],
+                rhs=x_codes[:, places].bitcast(FP8X4),
+                rhs_scale=x_plane[:, places],
+                start=True,
+                stop=True,
+            )
+            nc.scalar.activation(y[t][:, places], acc[:], RELU)
 
         w_codes = [keep.tile([P, N], U32, name="w_codes%d" % u, align_bytes=64) for u in range(1)]
         w_plane = [keep.tile([P, N], U8, name="w_plane%d" % u, align_bytes=64) for u in range(2)]
         w_bf = {}
 
         def cast_weights(cast, tag, u, c0, c1):
-            w_bf[u, c0] = keep.tile([P, (c1 - c0) * PACK], BF16, name="w_bf%d_%d" % (u, c0), tag=tag, align_bytes=64)
+            lead = 2 * CHUNKS[2] if u == 1 else 0
+            room = keep.tile([P, lead + (c1 - c0) * PACK], BF16, name="w_bf%d_%d" % (u, c0), tag=tag, align_bytes=64)
+            w_bf[u, c0] = room[:, lead:]
+            if u == 1:
+                looked_up[2] = room[:, : 8 * CHUNKS[2]].rearrange("p (t n) -> p t n", t=PACK)
             cast(
-                w_bf[u, c0][:].rearrange("p (c i j) -> p c j i", i=4, j=PACK),
+                w_bf[u, c0].rearrange("p (c i j) -> p c j i", i=4, j=PACK),
                 raw_piece(u, c0, c1).rearrange("p j (c i) -> p c j i", i=4),
             )
 
         def quantize_weights(u, c0, c1):
             if u == 1:
-                w_codes.append(keep.tile([P, N], U32, name="w_codes1", tag="z_bf0", align_bytes=64))
+                w_codes.append(keep.tile([P, N], U32, name="w_codes1", tag="w_codes1", align_bytes=64))
             nc.vector.quantize_mx(
-                out=w_codes[u][:, c0:c1].bitcast(FP8X4), scales=w_plane[u][:, c0:c1], in_=w_bf[u, c0][:]
+                out=w_codes[u][:, c0:c1].bitcast(FP8X4), scales=w_plane[u][:, c0:c1], in_=w_bf[u, c0]
             )
 
         out_rows = out.rearrange("(m p) v -> p m v", p=P)
         starts = [sum(CHUNKS[:c]) for c in range(len(CHUNKS))]
         looked_up, woven, z_bf, z_codes, z_plane = {}, {}, {}, {}, {}
 
-        def gather(c):
-            n = 2 * CHUNKS[c]
-            looked_up[c] = keep.tile([P, PACK, n], BF16, name="looked_up%d" % c, tag=("looked_up0", "w1_codes", "looked_up0")[c], align_bytes=64)
+        def gather(c, planes):
+            if c not in looked_up:
+                looked_up[c] = keep.tile([P, PACK, 2 * CHUNKS[c]], BF16, name="looked_up%d" % c, tag=("looked_up0", "w1_codes", "z_bf0")[c], align_bytes=64)
             entries = order_sb[:, starts[c] // 8 : (starts[c] + CHUNKS[c]) // 8]
-            for t in range(PACK):
+            for t in planes:
                 nc.vector.tensor_copy(looked_up[c][:, t, :], y[t][:].indirect(entries))
 
-        def weave(c):
+        def weave(c, parts):
             n = 2 * CHUNKS[c]
-            woven[c] = keep.tile([P, n * PACK], BF16, name="woven%d" % c, tag="late" if c == 1 else "woven%d" % c, align_bytes=64)
-            nc.scalar.copy(
-                woven[c][:].rearrange("p (c i t) -> p c t i", i=4, t=PACK),
-                looked_up[c][:].rearrange("p t (c i) -> p c t i", i=4),
-            )
+            woven[c] = keep.tile([P, n * PACK], BF16, name="woven%d" % c, tag=("woven0", "late", "z_codes0")[c], align_bytes=64)
+            groups = n // 4 // parts
+            for part in range(parts):
+                nc.scalar.copy(
+                    woven[c][:].rearrange("p (c i t) -> p c t i", i=4, t=PACK)[:, part * groups : (part + 1) * groups],
+                    looked_up[c][:, :, :].rearrange("p t (c i) -> p c t i", i=4)[:, part * groups : (part + 1) * groups],
+                )
 
-        def pool_pairs(c):
+        def pool_pairs(c, parts):
             width = CHUNKS[c] * PACK
-            z_bf[c] = keep.tile([P, 2 * width], BF16, name="z_bf%d" % c, tag="late" if c == 2 else "z_bf%d" % c, align_bytes=64)
-            for u, op in enumerate((MAX, MIN)):
-                pooled = z_bf[c][:, u * width : (u + 1) * width]
-                if c in woven:
-                    pairs = woven[c][:].rearrange("p (v s t) -> p s v t", s=2, t=PACK)
-                    dst = pooled.rearrange("p (v t) -> p v t", t=PACK)
-                else:
-                    pairs = looked_up[c][:].rearrange("p t (c i s) -> p s c t i", i=4, s=2)
-                    dst = pooled.rearrange("p (c i t) -> p c t i", i=4, t=PACK)
-                nc.vector.tensor_tensor(dst, pairs[:, 0], pairs[:, 1], op)
+            z_bf[c] = keep.tile([P, 2 * width], BF16, name="z_bf%d" % c, tag="z_bf%d" % min(c, 1), align_bytes=64)
+            pairs = woven[c][:].rearrange("p (v s t) -> p s v t", s=2, t=PACK)
+            pooled = z_bf[c][:].rearrange("p (u v t) -> p u v t", u=2, t=PACK)
+            for part in range(parts):
+                vs = slice(part * CHUNKS[c] // parts, (part + 1) * CHUNKS[c] // parts)
+                for u, op in enumerate((MAX, MIN)):
+                    nc.vector.tensor_tensor(pooled[:, u, vs], pairs[:, 0, vs], pairs[:, 1, vs], op)
 
         def quantize_pooled(c, calls):
-            z_codes[c] = keep.tile([P, 2 * CHUNKS[c]], U32, name="z_codes%d" % c, align_bytes=64)
+            z_codes[c] = keep.tile([P, 2 * CHUNKS[c]], U32, name="z_codes%d" % c, tag="z_codes%d" % c, align_bytes=64)
             z_plane[c] = keep.tile([P, 2 * CHUNKS[c]], U8, name="z_plane%d" % c, align_bytes=64)
             words = 2 * CHUNKS[c] // calls
             for i in range(calls):
@@ -180,31 +183,34 @@ def tile_picked_winmax_relu_p_kernel(tc, x_words, x_scales, w1, w2, w3, offs, or
                         start=(u == 0),
                         stop=(u == 1),
                     )
+            staged = keep.tile([P, 2, 2, CHUNKS[c]], F32, name="staged%d" % c, tag="staged%d" % c, align_bytes=64)
             for half in range(2):
-                staged = keep.tile([P, 2, CHUNKS[c]], F32, name="staged%d_%d" % (c, half), align_bytes=64)
                 for r in range(2):
-                    m = 2 * r + half
+                    m = 2 * r + half if last else 2 * half + r
                     leave = nc.vector.tensor_copy if last and half == 1 else nc.scalar.copy
-                    leave(staged[:, r, :], banks[m][:])
-                nc.sync.dma_start(out_rows[:, half::2, starts[c] : starts[c] + CHUNKS[c]], staged[:])
+                    leave(staged[:, half, r, :], banks[m][:])
+                queue = nc.scalar if last and half == 0 else nc.sync
+                queue.dma_start(out_rows[:, slice(half, 4, 2) if last else slice(2 * half, 2 * half + 2), starts[c] : starts[c] + CHUNKS[c]], staged[:, half])
 
         cast_weights(nc.vector.tensor_copy, "looked_up0", *pieces[0])
         quantize_weights(*pieces[0])
         cast_weights(nc.scalar.copy, "w1_codes", *pieces[1])
-        gather(0)
-        weave(0)
+        gather(0, range(PACK))
+        weave(0, 1)
         cast_weights(nc.scalar.copy, "looked_up0", *pieces[2])
         quantize_weights(*pieces[1])
-        gather(1)
-        weave(1)
-        pool_pairs(0)
+        gather(1, range(PACK))
+        weave(1, 1)
+        pool_pairs(0, 1)
         quantize_pooled(0, 1)
+        gather(2, (0,))
         quantize_weights(*pieces[2])
+        gather(2, (1, 2, 3))
         project(0)
-        gather(2)
-        pool_pairs(1)
+        weave(2, 2)
+        pool_pairs(1, 1)
         quantize_pooled(1, 1)
         project(1)
-        pool_pairs(2)
+        pool_pairs(2, 2)
         quantize_pooled(2, 2)
         project(2)

@@ -142,14 +142,14 @@ def tile_picked_winmax_relu_p_kernel(tc, x_words, x_scales, w1, w2, w3, offs, or
             groups = n // 4 // parts
             for part in range(parts):
                 nc.scalar.copy(
-                    woven[c][:].rearrange("p (c i t) -> p c t i", i=4, t=PACK)[:, part * groups : (part + 1) * groups],
-                    looked_up[c][:, :, :].rearrange("p t (c i) -> p c t i", i=4)[:, part * groups : (part + 1) * groups],
+                    woven[c][:].rearrange("p (s c i t) -> p c t i s", s=2, i=2, t=PACK)[:, part * groups : (part + 1) * groups],
+                    looked_up[c][:, :, :].rearrange("p t (c i s) -> p c t i s", i=2, s=2)[:, part * groups : (part + 1) * groups],
                 )
 
         def pool_pairs(c, parts):
             width = CHUNKS[c] * PACK
             z_bf[c] = keep.tile([P, 2 * width], BF16, name="z_bf%d" % c, tag="z_bf%d" % min(c, 1), align_bytes=64)
-            pairs = woven[c][:].rearrange("p (v s t) -> p s v t", s=2, t=PACK)
+            pairs = woven[c][:].rearrange("p (s v t) -> p s v t", s=2, t=PACK)
             pooled = z_bf[c][:].rearrange("p (u v t) -> p u v t", u=2, t=PACK)
             for part in range(parts):
                 vs = slice(part * CHUNKS[c] // parts, (part + 1) * CHUNKS[c] // parts)
@@ -171,8 +171,9 @@ def tile_picked_winmax_relu_p_kernel(tc, x_words, x_scales, w1, w2, w3, offs, or
         def project(c):
             last = c == len(CHUNKS) - 1
             banks = [psum.tile([P, CHUNKS[c]], F32, name="res", tag="bank%d" % (4 * (c % 2) + m)) for m in range(N // P)]
-            for u in range(2):
-                for m in range(N // P):
+            steps = [(u, m) for u in range(2) for m in range(N // P)]
+            for u, m in sorted(steps, key=lambda step: step[1]) if last else steps:
+                if True:
                     cols = slice(m * P, (m + 1) * P)
                     nc.tensor.matmul_mx(
                         out=banks[m][:],
@@ -183,14 +184,15 @@ def tile_picked_winmax_relu_p_kernel(tc, x_words, x_scales, w1, w2, w3, offs, or
                         start=(u == 0),
                         stop=(u == 1),
                     )
-            staged = keep.tile([P, 2, 2, CHUNKS[c]], F32, name="staged%d" % c, tag="staged%d" % c, align_bytes=64)
-            for half in range(2):
-                for r in range(2):
-                    m = 2 * r + half if last else 2 * half + r
-                    leave = nc.vector.tensor_copy if last and half == 1 else nc.scalar.copy
-                    leave(staged[:, half, r, :], banks[m][:])
-                queue = nc.scalar if last and half == 0 else nc.sync
-                queue.dma_start(out_rows[:, slice(half, 4, 2) if last else slice(2 * half, 2 * half + 2), starts[c] : starts[c] + CHUNKS[c]], staged[:, half])
+            staged = keep.tile([P, N // P, CHUNKS[c]], F32, name="staged%d" % c, align_bytes=64)
+            per_store = 1 if last else 2
+            for m in range(N // P):
+                by_vector = last and m % 2 == 1
+                (nc.vector.tensor_copy if by_vector else nc.scalar.copy)(staged[:, m, :], banks[m][:])
+                if (m + 1) % per_store == 0:
+                    ms = slice(m + 1 - per_store, m + 1)
+                    queue = nc.scalar if last and not by_vector else nc.sync
+                    queue.dma_start(out_rows[:, ms, starts[c] : starts[c] + CHUNKS[c]], staged[:, ms, :])
 
         cast_weights(nc.vector.tensor_copy, "looked_up0", *pieces[0])
         quantize_weights(*pieces[0])

@@ -15,12 +15,12 @@ FP8X4 = mybir.dt.float8_e4m3fn_x4
 RELU = mybir.ActivationFunctionType.Relu
 MAX = mybir.AluOpType.max
 MIN = mybir.AluOpType.min
+MULT = mybir.AluOpType.mult
+ADD = mybir.AluOpType.add
 
 P = 128
 PACK = 4
-BANK = 512
-CHUNKS = (256,128,128)
-WOVEN_BY_SCALAR = (0, 1)
+CHUNKS = (256, 128, 128)
 
 
 def tile_picked_winmax_relu_p_kernel(tc, x_words, x_scales, w1, w2, w3, offs, order, out):
@@ -52,23 +52,23 @@ def tile_picked_winmax_relu_p_kernel(tc, x_words, x_scales, w1, w2, w3, offs, or
         nc.scalar.activation(warm_out[:], warm_in[:], RELU)
         x_plane = keep.tile([P, S], U8, name="x_plane", align_bytes=64)
         nc.vector.memset(x_plane[:].bitcast(I32), 0)
-        picked_scales = keep.tile([P, S], U8, name="picked_scales", align_bytes=64)
+        picked_scales = keep.tile([P, S], U8, name="picked_scales", tag="picked", align_bytes=64)
         nc.vector.tensor_copy(picked_scales[:], scale_table[:].indirect(offs_sb[:]))
         for q in range(4):
             nc.sync.dma_start(
                 x_plane[32 * q : 32 * q + 4, :].bitcast(I32),
                 picked_scales[32 * q : 32 * q + 32 : 8, :].bitcast(I32),
             )
-        w_raw = keep.tile([P, 2 * PACK * N], F32, name="w_raw", tag="late", align_bytes=64)
-        pieces = ((0, 0, N // 2), (0, N // 2, N), (1, 0, N))
         w_rows = [w.rearrange("(p j) c -> p j c", j=PACK) for w in (w2, w3)]
+        half = N // 2
+        early_raw = keep.tile([P, 3 * PACK * half], F32, name="early_raw", tag="late", align_bytes=64)
+        raw = [early_raw[:, h * PACK * half : (h + 1) * PACK * half].rearrange("p (j c) -> p j c", j=PACK) for h in range(3)]
+        for h in range(3):
+            nc.sync.dma_start(raw[h], w_rows[h // 2][:, :, (h % 2) * half : (h % 2 + 1) * half])
+        last_raw = keep.tile([P, PACK, half], F32, name="last_raw", tag="picked", align_bytes=64)
+        nc.sync.dma_start(last_raw[:], w_rows[1][:, :, half:])
 
-        def raw_piece(u, c0, c1):
-            return w_raw[:, PACK * (u * N + c0) : PACK * (u * N + c1)].rearrange("p (j c) -> p j c", j=PACK)
-
-        for u, c0, c1 in pieces:
-            nc.sync.dma_start(raw_piece(u, c0, c1), w_rows[u][:, :, c0:c1])
-        x_codes = keep.tile([P, S], U32, name="x_codes", tag="x_codes", align_bytes=64)
+        x_codes = keep.tile([P, S], U32, name="x_codes", align_bytes=64)
         nc.vector.tensor_copy(x_codes[:], word_table[:].indirect(offs_sb[:]))
 
         w1_bf = keep.tile([P, PACK, P, PACK], BF16, name="w1_bf", align_bytes=64)
@@ -77,9 +77,9 @@ def tile_picked_winmax_relu_p_kernel(tc, x_words, x_scales, w1, w2, w3, offs, or
                 w1_bf[:, :, h * (P // 2) + m0 : h * (P // 2) + m1, :].rearrange("p t m j -> p m j t"),
                 w1_raw[h][:].rearrange("p j (m t) -> p m j t", t=PACK)[:, m0:m1],
             )
-        w1_codes = keep.tile([P, H], U32, name="w1_codes", tag="w1_codes", align_bytes=64)
+        w1_codes = keep.tile([P, H], U32, name="w1_codes", align_bytes=64)
         w1_plane = keep.tile([P, H], U8, name="w1_plane", align_bytes=64)
-        y = [keep.tile([P, S], F32, name="y%d" % t, tag="y%d" % t, align_bytes=64) for t in range(PACK)]
+        y = [keep.tile([P, S], F32, name="y%d" % t, align_bytes=64) for t in range(PACK)]
         for t0, t1 in ((0, 1), (1, 2), (2, 4)):
             cols = slice(t0 * P, t1 * P)
             nc.vector.quantize_mx(
@@ -87,43 +87,28 @@ def tile_picked_winmax_relu_p_kernel(tc, x_words, x_scales, w1, w2, w3, offs, or
                 scales=w1_plane[:, cols],
                 in_=w1_bf[:, t0:t1, :, :].rearrange("p t m j -> p (t m j)"),
             )
-        passes = [(t, s0, width) for t, width in enumerate((256, 512, 512, 512)) for s0 in range(0, S, width)]
-        for i, (t, s0, width) in enumerate(passes):
+        passes = [(t, s0, s0 + width) for t, width in enumerate((256, 512, 512, 512)) for s0 in range(0, S, width)]
+        for i, (t, s0, s1) in enumerate(passes):
             cols = slice(t * P, (t + 1) * P)
-            places = slice(s0, s0 + width)
-            acc = psum.tile([P, width], F32, name="acc", tag="bank%d" % (i % 8))
+            acc = psum.tile([P, s1 - s0], F32, name="acc", tag="bank%d" % (i % 8))
             nc.tensor.matmul_mx(
                 out=acc[:],
                 lhsT=w1_codes[:, cols].bitcast(FP8X4),
                 lhsT_scale=w1_plane[:, cols],
-                rhs=x_codes[:, places].bitcast(FP8X4),
-                rhs_scale=x_plane[:, places],
+                rhs=x_codes[:, s0:s1].bitcast(FP8X4),
+                rhs_scale=x_plane[:, s0:s1],
                 start=True,
                 stop=True,
             )
-            nc.scalar.activation(y[t][:, places], acc[:], RELU)
+            nc.scalar.activation(y[t][:, s0:s1], acc[:], RELU)
 
-        w_codes = [keep.tile([P, N], U32, name="w_codes%d" % u, align_bytes=64) for u in range(1)]
-        w_plane = [keep.tile([P, N], U8, name="w_plane%d" % u, align_bytes=64) for u in range(2)]
-        w_bf = {}
+        w_codes_all = keep.tile([P, 2 * N], U32, name="w_codes_all", align_bytes=64)
+        w_plane_all = keep.tile([P, 2 * N], U8, name="w_plane_all", align_bytes=64)
+        w_codes = [w_codes_all[:, u * N : (u + 1) * N] for u in range(2)]
+        w_plane = [w_plane_all[:, u * N : (u + 1) * N] for u in range(2)]
 
-        def cast_weights(cast, tag, u, c0, c1):
-            lead = 2 * CHUNKS[2] if u == 1 else 0
-            room = keep.tile([P, lead + (c1 - c0) * PACK], BF16, name="w_bf%d_%d" % (u, c0), tag=tag, align_bytes=64)
-            w_bf[u, c0] = room[:, lead:]
-            if u == 1:
-                looked_up[2] = room[:, : 8 * CHUNKS[2]].rearrange("p (t n) -> p t n", t=PACK)
-            cast(
-                w_bf[u, c0].rearrange("p (c i j) -> p c j i", i=4, j=PACK),
-                raw_piece(u, c0, c1).rearrange("p j (c i) -> p c j i", i=4),
-            )
-
-        def quantize_weights(u, c0, c1):
-            if u == 1:
-                w_codes.append(keep.tile([P, N], U32, name="w_codes1", tag="w_codes1", align_bytes=64))
-            nc.vector.quantize_mx(
-                out=w_codes[u][:, c0:c1].bitcast(FP8X4), scales=w_plane[u][:, c0:c1], in_=w_bf[u, c0]
-            )
+        def cast_weights(cast, bf, raw):
+            cast(bf.rearrange("p (c i j) -> p c j i", i=4, j=PACK), raw.rearrange("p j (c i) -> p c j i", i=4))
 
         out_rows = out.rearrange("(m p) v -> p m v", p=P)
         starts = [sum(CHUNKS[:c]) for c in range(len(CHUNKS))]
@@ -131,24 +116,25 @@ def tile_picked_winmax_relu_p_kernel(tc, x_words, x_scales, w1, w2, w3, offs, or
 
         def gather(c, planes):
             if c not in looked_up:
-                looked_up[c] = keep.tile([P, PACK, 2 * CHUNKS[c]], BF16, name="looked_up%d" % c, tag=("looked_up0", "w1_codes", "z_bf0")[c], align_bytes=64)
+                planes_tile = keep.tile([P, PACK, 2 * CHUNKS[c]], BF16, name="looked_up%d" % c, tag=("looked_up0", "late", "late")[c], align_bytes=64)
+                looked_up[c] = planes_tile[:]
             entries = order_sb[:, starts[c] // 8 : (starts[c] + CHUNKS[c]) // 8]
             for t in planes:
                 nc.vector.tensor_copy(looked_up[c][:, t, :], y[t][:].indirect(entries))
 
-        def weave(c, parts):
+        def weave(c, parts, tag):
             n = 2 * CHUNKS[c]
-            woven[c] = keep.tile([P, n * PACK], BF16, name="woven%d" % c, tag=("woven0", "late", "z_codes0")[c], align_bytes=64)
+            woven[c] = keep.tile([P, n * PACK], BF16, name="woven%d" % c, tag=tag, align_bytes=64)
             groups = n // 4 // parts
             for part in range(parts):
                 nc.scalar.copy(
                     woven[c][:].rearrange("p (s c i t) -> p c t i s", s=2, i=2, t=PACK)[:, part * groups : (part + 1) * groups],
-                    looked_up[c][:, :, :].rearrange("p t (c i s) -> p c t i s", i=2, s=2)[:, part * groups : (part + 1) * groups],
+                    looked_up[c].rearrange("p t (c i s) -> p c t i s", i=2, s=2)[:, part * groups : (part + 1) * groups],
                 )
 
         def pool_pairs(c, parts):
             width = CHUNKS[c] * PACK
-            z_bf[c] = keep.tile([P, 2 * width], BF16, name="z_bf%d" % c, tag="z_bf%d" % min(c, 1), align_bytes=64)
+            z_bf[c] = keep.tile([P, 2 * width], BF16, name="z_bf%d" % c, align_bytes=64)
             pairs = woven[c][:].rearrange("p (s v t) -> p s v t", s=2, t=PACK)
             pooled = z_bf[c][:].rearrange("p (u v t) -> p u v t", u=2, t=PACK)
             for part in range(parts):
@@ -170,10 +156,9 @@ def tile_picked_winmax_relu_p_kernel(tc, x_words, x_scales, w1, w2, w3, offs, or
 
         def project(c):
             last = c == len(CHUNKS) - 1
-            banks = [psum.tile([P, CHUNKS[c]], F32, name="res", tag="bank%d" % (4 * (c % 2) + m)) for m in range(N // P)]
-            steps = [(u, m) for u in range(2) for m in range(N // P)]
-            for u, m in sorted(steps, key=lambda step: step[1]) if last else steps:
-                if True:
+            banks = [psum.tile([P, CHUNKS[c]], F32, name="res", tag="bank%d" % (4 * ((c + 1) % 2) + m)) for m in range(N // P)]
+            for u in range(2):
+                for m in range(N // P):
                     cols = slice(m * P, (m + 1) * P)
                     nc.tensor.matmul_mx(
                         out=banks[m][:],
@@ -194,24 +179,38 @@ def tile_picked_winmax_relu_p_kernel(tc, x_words, x_scales, w1, w2, w3, offs, or
                     queue = nc.scalar if last and not by_vector else nc.sync
                     queue.dma_start(out_rows[:, ms, starts[c] : starts[c] + CHUNKS[c]], staged[:, ms, :])
 
-        cast_weights(nc.vector.tensor_copy, "looked_up0", *pieces[0])
-        quantize_weights(*pieces[0])
-        cast_weights(nc.scalar.copy, "w1_codes", *pieces[1])
+        w_bf = keep.tile([P, 2 * PACK * N], BF16, name="w_bf", align_bytes=64)
+        piece = N // 4
+
+        def cast_on_gpsimd(c0, raw):
+            bf = w_bf[:, c0 * PACK : (c0 + piece) * PACK].rearrange("p (c j) -> p c j", j=PACK)
+            nc.gpsimd.tensor_scalar(bf, raw.rearrange("p j c -> p c j"), 1.0, 0.0, MULT, ADD)
+
+        def quantize_weights(c0, c1):
+            nc.vector.quantize_mx(
+                out=w_codes_all[:, c0:c1].bitcast(FP8X4), scales=w_plane_all[:, c0:c1], in_=w_bf[:, PACK * c0 : PACK * c1]
+            )
+
+        cast_weights(nc.vector.tensor_copy, w_bf[:, : PACK * half], raw[0])
+        quantize_weights(0, half)
+        for i in (2, 3):
+            cast_on_gpsimd(i * piece, raw[i // 2][:, :, (i % 2) * piece : (i % 2 + 1) * piece])
+        for i in range(2):
+            cast_on_gpsimd(3 * half + i * piece, last_raw[:, :, i * piece : (i + 1) * piece])
+        cast_weights(nc.scalar.copy, w_bf[:, 2 * PACK * half : 3 * PACK * half], raw[2])
         gather(0, range(PACK))
-        weave(0, 1)
-        cast_weights(nc.scalar.copy, "looked_up0", *pieces[2])
-        quantize_weights(*pieces[1])
+        weave(0, 1, "woven0")
         gather(1, range(PACK))
-        weave(1, 1)
+        quantize_weights(half, N)
+        quantize_weights(N, 2 * N)
+        weave(1, 1, "woven1")
         pool_pairs(0, 1)
-        quantize_pooled(0, 1)
-        gather(2, (0,))
-        quantize_weights(*pieces[2])
-        gather(2, (1, 2, 3))
+        quantize_pooled(0, 2)
+        gather(2, range(PACK))
         project(0)
-        weave(2, 2)
+        weave(2, 2, "z_codes0")
         pool_pairs(1, 1)
-        quantize_pooled(1, 1)
+        quantize_pooled(1, 2)
         project(1)
         pool_pairs(2, 2)
         quantize_pooled(2, 2)

@@ -46,10 +46,6 @@ def tile_picked_winmax_relu_p_kernel(tc, x_words, x_scales, w1, w2, w3, offs, or
             nc.sync.dma_start(w1_raw[h][:], w1_rows[:, :, h * (H // 2) : (h + 1) * (H // 2)])
         nc.sync.dma_start(order_sb[:], order)
 
-        warm_in = keep.tile([P, 1], F32, name="warm_in")
-        warm_out = keep.tile([P, 1], F32, name="warm_out")
-        nc.gpsimd.memset(warm_in[:], 0.0)
-        nc.scalar.activation(warm_out[:], warm_in[:], RELU)
         x_plane = keep.tile([P, S], U8, name="x_plane", align_bytes=64)
         nc.vector.memset(x_plane[:].bitcast(I32), 0)
         picked_scales = keep.tile([P, S], U8, name="picked_scales", tag="picked", align_bytes=64)

@@ -57,12 +57,12 @@ def tile_picked_winmax_relu_p_kernel(tc, x_words, x_scales, w1, w2, w3, offs, or
             )
         w_rows = [w.rearrange("(p j) c -> p j c", j=PACK) for w in (w2, w3)]
         half = N // 2
-        early_raw = keep.tile([P, 3 * PACK * half], F32, name="early_raw", tag="late", align_bytes=64)
-        raw = [early_raw[:, h * PACK * half : (h + 1) * PACK * half].rearrange("p (j c) -> p j c", j=PACK) for h in range(3)]
-        for h in range(3):
-            nc.sync.dma_start(raw[h], w_rows[h // 2][:, :, (h % 2) * half : (h % 2 + 1) * half])
-        last_raw = keep.tile([P, PACK, half], F32, name="last_raw", tag="picked", align_bytes=64)
-        nc.sync.dma_start(last_raw[:], w_rows[1][:, :, half:])
+        w2_raw = keep.tile([P, PACK * N], F32, name="w2_raw", tag="late", align_bytes=64)
+        raw = [w2_raw[:, h * PACK * half : (h + 1) * PACK * half].rearrange("p (j c) -> p j c", j=PACK) for h in range(2)]
+        for h in range(2):
+            nc.sync.dma_start(raw[h], w_rows[0][:, :, h * half : (h + 1) * half])
+        w3_raw = keep.tile([P, PACK, N], F32, name="w3_raw", tag="picked", align_bytes=64)
+        nc.sync.dma_start(w3_raw[:], w_rows[1])
 
         x_codes = keep.tile([P, S], U32, name="x_codes", align_bytes=64)
         nc.vector.tensor_copy(x_codes[:], word_table[:].indirect(offs_sb[:]))
@@ -73,7 +73,7 @@ def tile_picked_winmax_relu_p_kernel(tc, x_words, x_scales, w1, w2, w3, offs, or
                 w1_bf[:, :, h * (P // 2) + m0 : h * (P // 2) + m1, :].rearrange("p t m j -> p m j t"),
                 w1_raw[h][:].rearrange("p j (m t) -> p m j t", t=PACK)[:, m0:m1],
             )
-        w1_codes = keep.tile([P, H], U32, name="w1_codes", align_bytes=64)
+        w1_codes = keep.tile([P, H], U32, name="w1_codes", tag="w1_codes", align_bytes=64)
         w1_plane = keep.tile([P, H], U8, name="w1_plane", align_bytes=64)
         y = [keep.tile([P, S], F32, name="y%d" % t, align_bytes=64) for t in range(PACK)]
         for t0, t1 in ((0, 1), (1, 2), (2, 4)):
@@ -83,7 +83,8 @@ def tile_picked_winmax_relu_p_kernel(tc, x_words, x_scales, w1, w2, w3, offs, or
                 scales=w1_plane[:, cols],
                 in_=w1_bf[:, t0:t1, :, :].rearrange("p t m j -> p (t m j)"),
             )
-        passes = [(t, s0, s0 + width) for t, width in enumerate((256, 512, 512, 512)) for s0 in range(0, S, width)]
+        widths = [(256, 256, 256, 128, 128), (256, 256, 256, 256), (512, 512), (512, 512)]
+        passes = [(t, sum(w[:i]), sum(w[: i + 1])) for t, w in enumerate(widths) for i in range(len(w))]
         for i, (t, s0, s1) in enumerate(passes):
             cols = slice(t * P, (t + 1) * P)
             acc = psum.tile([P, s1 - s0], F32, name="acc", tag="bank%d" % (i % 8))
@@ -96,12 +97,12 @@ def tile_picked_winmax_relu_p_kernel(tc, x_words, x_scales, w1, w2, w3, offs, or
                 start=True,
                 stop=True,
             )
-            nc.scalar.activation(y[t][:, s0:s1], acc[:], RELU)
+            if i == 2:
+                nc.vector.tensor_scalar_max(y[t][:, s0:s1], acc[:], 0.0)
+            else:
+                nc.scalar.activation(y[t][:, s0:s1], acc[:], RELU)
 
-        w_codes_all = keep.tile([P, 2 * N], U32, name="w_codes_all", align_bytes=64)
-        w_plane_all = keep.tile([P, 2 * N], U8, name="w_plane_all", align_bytes=64)
-        w_codes = [w_codes_all[:, u * N : (u + 1) * N] for u in range(2)]
-        w_plane = [w_plane_all[:, u * N : (u + 1) * N] for u in range(2)]
+        w_codes, w_plane = {}, {}
 
         def cast_weights(cast, bf, raw):
             cast(bf.rearrange("p (c i j) -> p c j i", i=4, j=PACK), raw.rearrange("p j (c i) -> p c j i", i=4))
@@ -128,26 +129,28 @@ def tile_picked_winmax_relu_p_kernel(tc, x_words, x_scales, w1, w2, w3, offs, or
                     looked_up[c].rearrange("p t (c i s) -> p c t i s", i=2, s=2)[:, part * groups : (part + 1) * groups],
                 )
 
-        def pool_pairs(c, parts):
+        def pool_pairs(c, parts, which=(0, 1)):
             width = CHUNKS[c] * PACK
-            z_bf[c] = keep.tile([P, 2 * width], BF16, name="z_bf%d" % c, align_bytes=64)
+            if c not in z_bf:
+                z_bf[c] = keep.tile([P, 2 * width], BF16, name="z_bf%d" % c, align_bytes=64)
             pairs = woven[c][:].rearrange("p (s v t) -> p s v t", s=2, t=PACK)
             pooled = z_bf[c][:].rearrange("p (u v t) -> p u v t", u=2, t=PACK)
             for part in range(parts):
                 vs = slice(part * CHUNKS[c] // parts, (part + 1) * CHUNKS[c] // parts)
-                for u, op in enumerate((MAX, MIN)):
-                    nc.vector.tensor_tensor(pooled[:, u, vs], pairs[:, 0, vs], pairs[:, 1, vs], op)
+                for u in which:
+                    nc.vector.tensor_tensor(pooled[:, u, vs], pairs[:, 0, vs], pairs[:, 1, vs], (MAX, MIN)[u])
 
-        def quantize_pooled(c, calls):
-            z_codes[c] = keep.tile([P, 2 * CHUNKS[c]], U32, name="z_codes%d" % c, tag="z_codes%d" % c, align_bytes=64)
-            z_plane[c] = keep.tile([P, 2 * CHUNKS[c]], U8, name="z_plane%d" % c, align_bytes=64)
-            words = 2 * CHUNKS[c] // calls
-            for i in range(calls):
-                cols = slice(i * words, (i + 1) * words)
+        def quantize_pooled(c, which):
+            if c not in z_codes:
+                z_codes[c] = keep.tile([P, 2 * CHUNKS[c]], U32, name="z_codes%d" % c, tag="z_codes%d" % c, align_bytes=64)
+                z_plane[c] = keep.tile([P, 2 * CHUNKS[c]], U8, name="z_plane%d" % c, align_bytes=64)
+            words = CHUNKS[c]
+            for u in which:
+                cols = slice(u * words, (u + 1) * words)
                 nc.vector.quantize_mx(
                     out=z_codes[c][:, cols].bitcast(FP8X4),
                     scales=z_plane[c][:, cols],
-                    in_=z_bf[c][:, PACK * i * words : PACK * (i + 1) * words],
+                    in_=z_bf[c][:, PACK * u * words : PACK * (u + 1) * words],
                 )
 
         def project(c):
@@ -155,11 +158,10 @@ def tile_picked_winmax_relu_p_kernel(tc, x_words, x_scales, w1, w2, w3, offs, or
             banks = [psum.tile([P, CHUNKS[c]], F32, name="res", tag="bank%d" % (4 * ((c + 1) % 2) + m)) for m in range(N // P)]
             for u in range(2):
                 for m in range(N // P):
-                    cols = slice(m * P, (m + 1) * P)
                     nc.tensor.matmul_mx(
                         out=banks[m][:],
-                        lhsT=w_codes[u][:, cols].bitcast(FP8X4),
-                        lhsT_scale=w_plane[u][:, cols],
+                        lhsT=w_codes[u * N + m * P].bitcast(FP8X4),
+                        lhsT_scale=w_plane[u * N + m * P],
                         rhs=z_codes[c][:, u * CHUNKS[c] : (u + 1) * CHUNKS[c]].bitcast(FP8X4),
                         rhs_scale=z_plane[c][:, u * CHUNKS[c] : (u + 1) * CHUNKS[c]],
                         start=(u == 0),
@@ -175,39 +177,49 @@ def tile_picked_winmax_relu_p_kernel(tc, x_words, x_scales, w1, w2, w3, offs, or
                     queue = nc.scalar if last and not by_vector else nc.sync
                     queue.dma_start(out_rows[:, ms, starts[c] : starts[c] + CHUNKS[c]], staged[:, ms, :])
 
-        w_bf = keep.tile([P, 2 * PACK * N], BF16, name="w_bf", align_bytes=64)
         piece = N // 4
 
-        def cast_on_gpsimd(c0, raw):
-            bf = w_bf[:, c0 * PACK : (c0 + piece) * PACK].rearrange("p (c j) -> p c j", j=PACK)
-            nc.gpsimd.tensor_scalar(bf, raw.rearrange("p j c -> p c j"), 1.0, 0.0, MULT, ADD)
+        def cast_on_gpsimd(bf, raw_piece):
+            nc.gpsimd.tensor_scalar(bf.rearrange("p (c j) -> p c j", j=PACK), raw_piece.rearrange("p j c -> p c j"), 1.0, 0.0, MULT, ADD)
 
-        def quantize_weights(c0, c1):
-            nc.vector.quantize_mx(
-                out=w_codes_all[:, c0:c1].bitcast(FP8X4), scales=w_plane_all[:, c0:c1], in_=w_bf[:, PACK * c0 : PACK * c1]
-            )
+        def weight_tiles(c0, c1, tag):
+            codes = keep.tile([P, c1 - c0], U32, name="w_codes%d" % c0, tag=tag, align_bytes=64)
+            plane = keep.tile([P, c1 - c0], U8, name="w_plane%d" % c0, align_bytes=64)
+            for c in range(c0, c1, P):
+                w_codes[c] = codes[:, c - c0 : c - c0 + P]
+                w_plane[c] = plane[:, c - c0 : c - c0 + P]
+            return codes, plane
 
-        cast_weights(nc.vector.tensor_copy, w_bf[:, : PACK * half], raw[0])
-        quantize_weights(0, half)
-        for i in (2, 3):
-            cast_on_gpsimd(i * piece, raw[i // 2][:, :, (i % 2) * piece : (i % 2 + 1) * piece])
-        for i in range(2):
-            cast_on_gpsimd(3 * half + i * piece, last_raw[:, :, i * piece : (i + 1) * piece])
-        cast_weights(nc.scalar.copy, w_bf[:, 2 * PACK * half : 3 * PACK * half], raw[2])
+        def quantize_weights(tiles, c0, bf):
+            codes, plane = tiles
+            nc.vector.quantize_mx(out=codes[:, c0 : c0 + half].bitcast(FP8X4), scales=plane[:, c0 : c0 + half], in_=bf)
+
+        w2_bf = [keep.tile([P, PACK * half], BF16, name="w2_bf%d" % h, tag=("w2_bf0", "w1_codes")[h], align_bytes=64) for h in range(2)]
+        w3_bf = keep.tile([P, PACK * N], BF16, name="w3_bf", align_bytes=64)
+        cast_weights(nc.vector.tensor_copy, w2_bf[0][:], raw[0])
+        quantize_weights(weight_tiles(0, half, "w2_codes0"), 0, w2_bf[0][:])
+        cast_on_gpsimd(w2_bf[1][:, : PACK * piece], raw[1][:, :, :piece])
+        for i in range(4):
+            cast_on_gpsimd(w3_bf[:, PACK * i * piece : PACK * (i + 1) * piece], w3_raw[:, :, i * piece : (i + 1) * piece])
+        cast_weights(nc.scalar.copy, w2_bf[1][:, PACK * piece :], raw[1][:, :, piece:])
         gather(0, range(PACK))
         weave(0, 1, "woven0")
         gather(1, range(PACK))
-        quantize_weights(half, N)
-        quantize_weights(N, 2 * N)
+        quantize_weights(weight_tiles(half, N, "w2_codes1"), 0, w2_bf[1][:])
         weave(1, 1, "woven1")
-        pool_pairs(0, 1)
-        quantize_pooled(0, 2)
+        pool_pairs(0, 1, (0,))
+        w3_tiles = weight_tiles(N, 2 * N, "looked_up0")
+        quantize_weights(w3_tiles, 0, w3_bf[:, : PACK * half])
+        quantize_pooled(0, (0,))
+        pool_pairs(0, 1, (1,))
+        quantize_weights(w3_tiles, half, w3_bf[:, PACK * half :])
+        quantize_pooled(0, (1,))
         gather(2, range(PACK))
         project(0)
         weave(2, 2, "z_codes0")
         pool_pairs(1, 1)
-        quantize_pooled(1, 2)
+        quantize_pooled(1, (0, 1))
         project(1)
         pool_pairs(2, 2)
-        quantize_pooled(2, 2)
+        quantize_pooled(2, (0, 1))
         project(2)

@@ -111,13 +111,14 @@ def tile_picked_winmax_relu_p_kernel(tc, x_words, x_scales, w1, w2, w3, offs, or
         starts = [sum(CHUNKS[:c]) for c in range(len(CHUNKS))]
         looked_up, woven, z_bf, z_codes, z_plane = {}, {}, {}, {}, {}
 
-        def gather(c, planes):
-            if c not in looked_up:
-                planes_tile = keep.tile([P, PACK, 2 * CHUNKS[c]], BF16, name="looked_up%d" % c, tag=("looked_up0", "late", "late")[c], align_bytes=64)
-                looked_up[c] = planes_tile[:]
-            entries = order_sb[:, starts[c] // 8 : (starts[c] + CHUNKS[c]) // 8]
-            for t in planes:
-                nc.vector.tensor_copy(looked_up[c][:, t, :], y[t][:].indirect(entries))
+        def gather(h, tag):
+            planes = keep.tile([P, PACK, V], BF16, name="looked_up%d" % h, tag=tag, align_bytes=64)
+            for t in range(PACK):
+                nc.vector.tensor_copy(planes[:, t, :], y[t][:].indirect(order_sb[:, h * V // 16 : (h + 1) * V // 16]))
+            for c in range(len(CHUNKS)):
+                e0 = 2 * starts[c] - h * V
+                if 0 <= e0 < V:
+                    looked_up[c] = planes[:, :, e0 : e0 + 2 * CHUNKS[c]]
 
         def weave(c, parts, tag):
             n = 2 * CHUNKS[c]
@@ -132,7 +133,7 @@ def tile_picked_winmax_relu_p_kernel(tc, x_words, x_scales, w1, w2, w3, offs, or
         def pool_pairs(c, parts, which=(0, 1)):
             width = CHUNKS[c] * PACK
             if c not in z_bf:
-                z_bf[c] = keep.tile([P, 2 * width], BF16, name="z_bf%d" % c, align_bytes=64)
+                z_bf[c] = keep.tile([P, 2 * width], BF16, name="z_bf%d" % c, tag=("z_bf0", "w3_bf", "z_bf2")[c], align_bytes=64)
             pairs = woven[c][:].rearrange("p (s v t) -> p s v t", s=2, t=PACK)
             pooled = z_bf[c][:].rearrange("p (u v t) -> p u v t", u=2, t=PACK)
             for part in range(parts):
@@ -168,7 +169,7 @@ def tile_picked_winmax_relu_p_kernel(tc, x_words, x_scales, w1, w2, w3, offs, or
                         stop=(u == 1),
                     )
             staged = keep.tile([P, N // P, CHUNKS[c]], F32, name="staged%d" % c, align_bytes=64)
-            per_store = 1 if last else 2
+            per_store = 2 if c == 1 else 1
             for m in range(N // P):
                 by_vector = last and m % 2 == 1
                 (nc.vector.tensor_copy if by_vector else nc.scalar.copy)(staged[:, m, :], banks[m][:])
@@ -195,31 +196,30 @@ def tile_picked_winmax_relu_p_kernel(tc, x_words, x_scales, w1, w2, w3, offs, or
             nc.vector.quantize_mx(out=codes[:, c0 : c0 + half].bitcast(FP8X4), scales=plane[:, c0 : c0 + half], in_=bf)
 
         w2_bf = [keep.tile([P, PACK * half], BF16, name="w2_bf%d" % h, tag=("w2_bf0", "w1_codes")[h], align_bytes=64) for h in range(2)]
-        w3_bf = keep.tile([P, PACK * N], BF16, name="w3_bf", align_bytes=64)
+        w3_bf = keep.tile([P, PACK * N], BF16, name="w3_bf", tag="w3_bf", align_bytes=64)
         cast_weights(nc.vector.tensor_copy, w2_bf[0][:], raw[0])
         quantize_weights(weight_tiles(0, half, "w2_codes0"), 0, w2_bf[0][:])
         cast_on_gpsimd(w2_bf[1][:, : PACK * piece], raw[1][:, :, :piece])
         for i in range(4):
             cast_on_gpsimd(w3_bf[:, PACK * i * piece : PACK * (i + 1) * piece], w3_raw[:, :, i * piece : (i + 1) * piece])
         cast_weights(nc.scalar.copy, w2_bf[1][:, PACK * piece :], raw[1][:, :, piece:])
-        gather(0, range(PACK))
+        gather(0, "looked_up0")
         weave(0, 1, "woven0")
-        gather(1, range(PACK))
-        quantize_weights(weight_tiles(half, N, "w2_codes1"), 0, w2_bf[1][:])
+        gather(1, "late")
         weave(1, 1, "woven1")
+        weave(2, 1, "woven2")
         pool_pairs(0, 1, (0,))
-        w3_tiles = weight_tiles(N, 2 * N, "looked_up0")
-        quantize_weights(w3_tiles, 0, w3_bf[:, : PACK * half])
+        quantize_weights(weight_tiles(half, N, "w2_codes1"), 0, w2_bf[1][:])
         quantize_pooled(0, (0,))
         pool_pairs(0, 1, (1,))
+        w3_tiles = weight_tiles(N, 2 * N, "looked_up0")
+        quantize_weights(w3_tiles, 0, w3_bf[:, : PACK * half])
         quantize_weights(w3_tiles, half, w3_bf[:, PACK * half :])
         quantize_pooled(0, (1,))
-        gather(2, range(PACK))
         project(0)
-        weave(2, 2, "z_codes0")
         pool_pairs(1, 1)
         quantize_pooled(1, (0, 1))
         project(1)
-        pool_pairs(2, 2)
+        pool_pairs(2, 1)
         quantize_pooled(2, (0, 1))
         project(2)

@@ -20,7 +20,7 @@ ADD = mybir.AluOpType.add
 
 P = 128
 PACK = 4
-CHUNKS = (256, 128, 128)
+CHUNK = 128
 
 
 def tile_picked_winmax_relu_p_kernel(tc, x_words, x_scales, w1, w2, w3, offs, order, out):
@@ -35,16 +35,14 @@ def tile_picked_winmax_relu_p_kernel(tc, x_words, x_scales, w1, w2, w3, offs, or
         word_table = keep.tile([P, T], U32, name="word_table", align_bytes=64)
         w1_raw = [keep.tile([P, PACK, H // 2], F32, name="w1_raw%d" % h, align_bytes=64) for h in range(2)]
 
+        nc.vector.memset(scale_table[:].bitcast(I32), 0)
         nc.sync.dma_start(offs_sb[:], offs)
-        nc.sync.dma_start(
-            scale_table[:].bitcast(I32),
-            x_scales[0].bitcast(I32).unsqueeze(1).to_broadcast([16, 8, T // 4]),
-        )
+        nc.sync.dma_start(order_sb[:], order)
+        nc.sync.dma_start(scale_table[0:P:8, :].bitcast(I32), x_scales[0].bitcast(I32))
         nc.sync.dma_start(word_table[:].bitcast(I32), x_words[0].rearrange("p c r -> p (c r)").bitcast(I32))
         w1_rows = w1.rearrange("(p j) c -> p j c", j=PACK)
         for h in range(2):
             nc.sync.dma_start(w1_raw[h][:], w1_rows[:, :, h * (H // 2) : (h + 1) * (H // 2)])
-        nc.sync.dma_start(order_sb[:], order)
 
         x_plane = keep.tile([P, S], U8, name="x_plane", align_bytes=64)
         nc.vector.memset(x_plane[:].bitcast(I32), 0)
@@ -102,124 +100,122 @@ def tile_picked_winmax_relu_p_kernel(tc, x_words, x_scales, w1, w2, w3, offs, or
             else:
                 nc.scalar.activation(y[t][:, s0:s1], acc[:], RELU)
 
-        w_codes, w_plane = {}, {}
-
-        def cast_weights(cast, bf, raw):
-            cast(bf.rearrange("p (c i j) -> p c j i", i=4, j=PACK), raw.rearrange("p j (c i) -> p c j i", i=4))
-
+        piece = N // 4
         out_rows = out.rearrange("(m p) v -> p m v", p=P)
-        starts = [sum(CHUNKS[:c]) for c in range(len(CHUNKS))]
         looked_up, woven, z_bf, z_codes, z_plane = {}, {}, {}, {}, {}
 
         def gather(h, tag):
-            planes = keep.tile([P, PACK, V], BF16, name="looked_up%d" % h, tag=tag, align_bytes=64)
+            looked_up[h] = keep.tile([P, PACK, V], BF16, name="looked_up%d" % h, tag=tag, align_bytes=64)
             for t in range(PACK):
-                nc.vector.tensor_copy(planes[:, t, :], y[t][:].indirect(order_sb[:, h * V // 16 : (h + 1) * V // 16]))
-            for c in range(len(CHUNKS)):
-                e0 = 2 * starts[c] - h * V
-                if 0 <= e0 < V:
-                    looked_up[c] = planes[:, :, e0 : e0 + 2 * CHUNKS[c]]
+                nc.vector.tensor_copy(looked_up[h][:, t, :], y[t][:].indirect(order_sb[:, h * V // 16 : (h + 1) * V // 16]))
 
-        def weave(c, parts, tag):
-            n = 2 * CHUNKS[c]
-            woven[c] = keep.tile([P, n * PACK], BF16, name="woven%d" % c, tag=tag, align_bytes=64)
-            groups = n // 4 // parts
-            for part in range(parts):
-                nc.scalar.copy(
-                    woven[c][:].rearrange("p (s c i t) -> p c t i s", s=2, i=2, t=PACK)[:, part * groups : (part + 1) * groups],
-                    looked_up[c].rearrange("p t (c i s) -> p c t i s", i=2, s=2)[:, part * groups : (part + 1) * groups],
-                )
+        def weave(c0, c1):
+            pairs = (c1 - c0) * CHUNK
+            tile = keep.tile([P, 2 * pairs * PACK], BF16, name="woven%d" % c0, align_bytes=64)
+            e0 = 2 * CHUNK * (c0 % 2)
+            nc.scalar.copy(
+                tile[:].rearrange("p (s c i t) -> p c t i s", s=2, i=2, t=PACK),
+                looked_up[c0 // 2][:, :, e0 : e0 + 2 * pairs].rearrange("p t (c i s) -> p c t i s", i=2, s=2),
+            )
+            for c in range(c0, c1):
+                woven[c] = tile[:].rearrange("p (s e) -> p s e", s=2)[:, :, (c - c0) * CHUNK * PACK : (c - c0 + 1) * CHUNK * PACK]
 
-        def pool_pairs(c, parts, which=(0, 1)):
-            width = CHUNKS[c] * PACK
+        def pool_pairs(c, which):
             if c not in z_bf:
-                z_bf[c] = keep.tile([P, 2 * width], BF16, name="z_bf%d" % c, tag=("z_bf0", "w3_bf", "z_bf2")[c], align_bytes=64)
-            pairs = woven[c][:].rearrange("p (s v t) -> p s v t", s=2, t=PACK)
-            pooled = z_bf[c][:].rearrange("p (u v t) -> p u v t", u=2, t=PACK)
-            for part in range(parts):
-                vs = slice(part * CHUNKS[c] // parts, (part + 1) * CHUNKS[c] // parts)
-                for u in which:
-                    nc.vector.tensor_tensor(pooled[:, u, vs], pairs[:, 0, vs], pairs[:, 1, vs], (MAX, MIN)[u])
-
-        def quantize_pooled(c, which):
-            if c not in z_codes:
-                z_codes[c] = keep.tile([P, 2 * CHUNKS[c]], U32, name="z_codes%d" % c, tag="z_codes%d" % c, align_bytes=64)
-                z_plane[c] = keep.tile([P, 2 * CHUNKS[c]], U8, name="z_plane%d" % c, align_bytes=64)
-            words = CHUNKS[c]
+                z_bf[c] = keep.tile([P, 2, CHUNK * PACK], BF16, name="z_bf%d" % c, tag=("z_bf0", "w3_bf", "z_bf0", "z_bf3")[c], align_bytes=64)
             for u in which:
-                cols = slice(u * words, (u + 1) * words)
-                nc.vector.quantize_mx(
-                    out=z_codes[c][:, cols].bitcast(FP8X4),
-                    scales=z_plane[c][:, cols],
-                    in_=z_bf[c][:, PACK * u * words : PACK * (u + 1) * words],
-                )
+                nc.vector.tensor_tensor(z_bf[c][:, u, :], woven[c][:, 0, :], woven[c][:, 1, :], (MAX, MIN)[u])
+
+        def quantize_pooled(c, u0, u1):
+            if c not in z_codes:
+                z_codes[c] = keep.tile([P, 2 * CHUNK], U32, name="z_codes%d" % c, align_bytes=64)
+                z_plane[c] = keep.tile([P, 2 * CHUNK], U8, name="z_plane%d" % c, align_bytes=64)
+            cols = slice(u0 * CHUNK, u1 * CHUNK)
+            nc.vector.quantize_mx(
+                out=z_codes[c][:, cols].bitcast(FP8X4),
+                scales=z_plane[c][:, cols],
+                in_=z_bf[c][:, u0:u1, :].rearrange("p u e -> p (u e)"),
+            )
+
+        def one_pass(res, c, u, m):
+            codes, plane, c0 = (early_codes, early_plane, 0) if u * N + m * P < half else (w_codes, w_plane, half)
+            w_cols = slice(u * N + m * P - c0, u * N + (m + 1) * P - c0)
+            z_cols = slice(u * CHUNK, (u + 1) * CHUNK)
+            nc.tensor.matmul_mx(
+                out=res,
+                lhsT=codes[:, w_cols].bitcast(FP8X4),
+                lhsT_scale=plane[:, w_cols],
+                rhs=z_codes[c][:, z_cols].bitcast(FP8X4),
+                rhs_scale=z_plane[c][:, z_cols],
+                start=(u == 0),
+                stop=(u == 1),
+            )
 
         def project(c):
-            last = c == len(CHUNKS) - 1
-            banks = [psum.tile([P, CHUNKS[c]], F32, name="res", tag="bank%d" % (4 * ((c + 1) % 2) + m)) for m in range(N // P)]
+            staged = keep.tile([P, N // P, CHUNK], F32, name="staged%d" % c, align_bytes=64)
+            vs = slice(c * CHUNK, (c + 1) * CHUNK)
+            for b in range(2):
+                bank = psum.tile([P, 2, CHUNK], F32, name="res", tag="bank%d" % (2 * c + b))
+                for i in range(2):
+                    for u in range(2):
+                        one_pass(bank[:, i, :], c, u, 2 * b + i)
+                ms = slice(2 * b, 2 * b + 2)
+                nc.scalar.copy(staged[:, ms, :], bank[:])
+                nc.sync.dma_start(out_rows[:, ms, vs], staged[:, ms, :])
+
+        def project_last(c):
+            staged = keep.tile([P, N // P, CHUNK], F32, name="staged%d" % c, align_bytes=64)
+            vs = slice(c * CHUNK, (c + 1) * CHUNK)
+            banks = [psum.tile([P, CHUNK], F32, name="res", tag="bank%d" % ((2 * c + m) % 8)) for m in range(N // P)]
             for u in range(2):
                 for m in range(N // P):
-                    nc.tensor.matmul_mx(
-                        out=banks[m][:],
-                        lhsT=w_codes[u * N + m * P].bitcast(FP8X4),
-                        lhsT_scale=w_plane[u * N + m * P],
-                        rhs=z_codes[c][:, u * CHUNKS[c] : (u + 1) * CHUNKS[c]].bitcast(FP8X4),
-                        rhs_scale=z_plane[c][:, u * CHUNKS[c] : (u + 1) * CHUNKS[c]],
-                        start=(u == 0),
-                        stop=(u == 1),
-                    )
-            staged = keep.tile([P, N // P, CHUNKS[c]], F32, name="staged%d" % c, align_bytes=64)
-            per_store = 2 if c == 1 else 1
+                    one_pass(banks[m][:], c, u, m)
             for m in range(N // P):
-                by_vector = last and m % 2 == 1
+                by_vector = m % 2 == 1
                 (nc.vector.tensor_copy if by_vector else nc.scalar.copy)(staged[:, m, :], banks[m][:])
-                if (m + 1) % per_store == 0:
-                    ms = slice(m + 1 - per_store, m + 1)
-                    queue = nc.scalar if last and not by_vector else nc.sync
-                    queue.dma_start(out_rows[:, ms, starts[c] : starts[c] + CHUNKS[c]], staged[:, ms, :])
-
-        piece = N // 4
+                (nc.sync if by_vector else nc.scalar).dma_start(out_rows[:, m : m + 1, vs], staged[:, m : m + 1, :])
 
         def cast_on_gpsimd(bf, raw_piece):
             nc.gpsimd.tensor_scalar(bf.rearrange("p (c j) -> p c j", j=PACK), raw_piece.rearrange("p j c -> p c j"), 1.0, 0.0, MULT, ADD)
 
-        def weight_tiles(c0, c1, tag):
-            codes = keep.tile([P, c1 - c0], U32, name="w_codes%d" % c0, tag=tag, align_bytes=64)
-            plane = keep.tile([P, c1 - c0], U8, name="w_plane%d" % c0, align_bytes=64)
-            for c in range(c0, c1, P):
-                w_codes[c] = codes[:, c - c0 : c - c0 + P]
-                w_plane[c] = plane[:, c - c0 : c - c0 + P]
-            return codes, plane
-
-        def quantize_weights(tiles, c0, bf):
-            codes, plane = tiles
-            nc.vector.quantize_mx(out=codes[:, c0 : c0 + half].bitcast(FP8X4), scales=plane[:, c0 : c0 + half], in_=bf)
+        def quantize_weights(c0, bf):
+            nc.vector.quantize_mx(out=w_codes[:, c0 : c0 + half].bitcast(FP8X4), scales=w_plane[:, c0 : c0 + half], in_=bf)
 
         w2_bf = [keep.tile([P, PACK * half], BF16, name="w2_bf%d" % h, tag=("w2_bf0", "w1_codes")[h], align_bytes=64) for h in range(2)]
         w3_bf = keep.tile([P, PACK * N], BF16, name="w3_bf", tag="w3_bf", align_bytes=64)
-        cast_weights(nc.vector.tensor_copy, w2_bf[0][:], raw[0])
-        quantize_weights(weight_tiles(0, half, "w2_codes0"), 0, w2_bf[0][:])
+        nc.vector.tensor_copy(
+            w2_bf[0][:].rearrange("p (c i j) -> p c j i", i=4, j=PACK), raw[0].rearrange("p j (c i) -> p c j i", i=4)
+        )
+        early_codes = keep.tile([P, half], U32, name="early_codes", align_bytes=64)
+        early_plane = keep.tile([P, half], U8, name="early_plane", align_bytes=64)
+        nc.vector.quantize_mx(out=early_codes[:].bitcast(FP8X4), scales=early_plane[:], in_=w2_bf[0][:])
         cast_on_gpsimd(w2_bf[1][:, : PACK * piece], raw[1][:, :, :piece])
         for i in range(4):
             cast_on_gpsimd(w3_bf[:, PACK * i * piece : PACK * (i + 1) * piece], w3_raw[:, :, i * piece : (i + 1) * piece])
-        cast_weights(nc.scalar.copy, w2_bf[1][:, PACK * piece :], raw[1][:, :, piece:])
+        nc.scalar.copy(
+            w2_bf[1][:, PACK * piece :].rearrange("p (c i j) -> p c j i", i=4, j=PACK),
+            raw[1][:, :, piece:].rearrange("p j (c i) -> p c j i", i=4),
+        )
         gather(0, "looked_up0")
-        weave(0, 1, "woven0")
+        weave(0, 2)
         gather(1, "late")
-        weave(1, 1, "woven1")
-        weave(2, 1, "woven2")
-        pool_pairs(0, 1, (0,))
-        quantize_weights(weight_tiles(half, N, "w2_codes1"), 0, w2_bf[1][:])
-        quantize_pooled(0, (0,))
-        pool_pairs(0, 1, (1,))
-        w3_tiles = weight_tiles(N, 2 * N, "looked_up0")
-        quantize_weights(w3_tiles, 0, w3_bf[:, : PACK * half])
-        quantize_weights(w3_tiles, half, w3_bf[:, PACK * half :])
-        quantize_pooled(0, (1,))
+        weave(2, 3)
+        weave(3, 4)
+        w_codes = keep.tile([P, 2 * N - half], U32, name="w_codes", tag="looked_up0", align_bytes=64)
+        w_plane = keep.tile([P, 2 * N - half], U8, name="w_plane", align_bytes=64)
+        pool_pairs(0, (0,))
+        quantize_weights(0, w2_bf[1][:])
+        quantize_pooled(0, 0, 1)
+        pool_pairs(0, (1,))
+        quantize_weights(half, w3_bf[:, : PACK * half])
+        quantize_weights(N, w3_bf[:, PACK * half :])
+        quantize_pooled(0, 1, 2)
         project(0)
-        pool_pairs(1, 1)
-        quantize_pooled(1, (0, 1))
-        project(1)
-        pool_pairs(2, 1)
-        quantize_pooled(2, (0, 1))
-        project(2)
+        for c in (1, 2):
+            pool_pairs(c, (0, 1))
+            quantize_pooled(c, 0, 2)
+            project(c)
+        pool_pairs(3, (0, 1))
+        quantize_pooled(3, 0, 1)
+        quantize_pooled(3, 1, 2)
+        project_last(3)

@@ -27,6 +27,7 @@ def tile_picked_winmax_relu_p_kernel(tc, x_words, x_scales, w1, w2, w3, offs, or
     nc = tc.nc
     with ExitStack() as ctx:
         keep = ctx.enter_context(tc.tile_pool(name="keep", bufs=1))
+        shared = ctx.enter_context(tc.tile_pool(name="shared", bufs=1))
         psum = ctx.enter_context(tc.psum_pool(name="psum", bufs=1))
 
         offs_sb = keep.tile([P, S // 16], U16, name="offs_sb")
@@ -54,13 +55,17 @@ def tile_picked_winmax_relu_p_kernel(tc, x_words, x_scales, w1, w2, w3, offs, or
                 picked_scales[32 * q : 32 * q + 32 : 8, :].bitcast(I32),
             )
         w_rows = [w.rearrange("(p j) c -> p j c", j=PACK) for w in (w2, w3)]
-        half = N // 2
-        w2_raw = keep.tile([P, PACK * N], F32, name="w2_raw", tag="late", align_bytes=64)
-        raw = [w2_raw[:, h * PACK * half : (h + 1) * PACK * half].rearrange("p (j c) -> p j c", j=PACK) for h in range(2)]
-        for h in range(2):
-            nc.sync.dma_start(raw[h], w_rows[0][:, :, h * half : (h + 1) * half])
-        w3_raw = keep.tile([P, PACK, N], F32, name="w3_raw", tag="picked", align_bytes=64)
-        nc.sync.dma_start(w3_raw[:], w_rows[1])
+        half, piece = N // 2, N // 4
+        w2_raw = keep.tile([P, PACK * 3 * piece], F32, name="w2_raw", tag="late", align_bytes=64)
+        w2_first_raw = w2_raw[:, : PACK * half].rearrange("p (j c) -> p j c", j=PACK)
+        w2_third_raw = w2_raw[:, PACK * half :].rearrange("p (j c) -> p j c", j=PACK)
+        nc.sync.dma_start(w2_first_raw, w_rows[0][:, :, :half])
+        nc.sync.dma_start(w2_third_raw, w_rows[0][:, :, half : 3 * piece])
+        last_raw = keep.tile([P, PACK * (N + piece)], F32, name="last_raw", tag="picked", align_bytes=64)
+        w3_raw = last_raw[:, : PACK * N].rearrange("p (j c) -> p j c", j=PACK)
+        w2_last_raw = last_raw[:, PACK * N :].rearrange("p (j c) -> p j c", j=PACK)
+        nc.sync.dma_start(w3_raw, w_rows[1])
+        nc.sync.dma_start(w2_last_raw, w_rows[0][:, :, 3 * piece :])
 
         x_codes = keep.tile([P, S], U32, name="x_codes", align_bytes=64)
         nc.vector.tensor_copy(x_codes[:], word_table[:].indirect(offs_sb[:]))
@@ -100,25 +105,23 @@ def tile_picked_winmax_relu_p_kernel(tc, x_words, x_scales, w1, w2, w3, offs, or
             else:
                 nc.scalar.activation(y[t][:, s0:s1], acc[:], RELU)
 
-        piece = N // 4
         out_rows = out.rearrange("(m p) v -> p m v", p=P)
         looked_up, woven, z_bf, z_codes, z_plane = {}, {}, {}, {}, {}
 
-        def gather(h, tag):
-            looked_up[h] = keep.tile([P, PACK, V], BF16, name="looked_up%d" % h, tag=tag, align_bytes=64)
+        def gather(h, planes):
+            looked_up[h] = planes
             for t in range(PACK):
                 nc.vector.tensor_copy(looked_up[h][:, t, :], y[t][:].indirect(order_sb[:, h * V // 16 : (h + 1) * V // 16]))
 
-        def weave(c0, c1):
-            pairs = (c1 - c0) * CHUNK
-            tile = keep.tile([P, 2 * pairs * PACK], BF16, name="woven%d" % c0, align_bytes=64)
-            e0 = 2 * CHUNK * (c0 % 2)
-            nc.scalar.copy(
-                tile[:].rearrange("p (s c i t) -> p c t i s", s=2, i=2, t=PACK),
-                looked_up[c0 // 2][:, :, e0 : e0 + 2 * pairs].rearrange("p t (c i s) -> p c t i s", i=2, s=2),
-            )
-            for c in range(c0, c1):
-                woven[c] = tile[:].rearrange("p (s e) -> p s e", s=2)[:, :, (c - c0) * CHUNK * PACK : (c - c0 + 1) * CHUNK * PACK]
+        def weave(h, parts, tag):
+            tile = keep.tile([P, parts, 2, V * PACK // (2 * parts)], BF16, name="woven%d" % h, tag=tag, align_bytes=64)
+            for part in range(parts):
+                nc.scalar.copy(
+                    tile[:, part].rearrange("p s (c i t) -> p c t i s", i=2, t=PACK),
+                    looked_up[h][:, :, part * V // parts : (part + 1) * V // parts].rearrange("p t (c i s) -> p c t i s", i=2, s=2),
+                )
+            for i in range(2):
+                woven[2 * h + i] = tile[:, i] if parts == 2 else tile[:, 0, :, i * CHUNK * PACK : (i + 1) * CHUNK * PACK]
 
         def pool_pairs(c, which):
             if c not in z_bf:
@@ -151,11 +154,11 @@ def tile_picked_winmax_relu_p_kernel(tc, x_words, x_scales, w1, w2, w3, offs, or
                 stop=(u == 1),
             )
 
-        def project(c):
+        def project_by_tile(c, bank0):
             staged = keep.tile([P, N // P, CHUNK], F32, name="staged%d" % c, align_bytes=64)
             vs = slice(c * CHUNK, (c + 1) * CHUNK)
             for b in range(2):
-                bank = psum.tile([P, 2, CHUNK], F32, name="res", tag="bank%d" % (2 * c + b))
+                bank = psum.tile([P, 2, CHUNK], F32, name="res", tag="bank%d" % (bank0 + b))
                 for i in range(2):
                     for u in range(2):
                         one_pass(bank[:, i, :], c, u, 2 * b + i)
@@ -163,59 +166,67 @@ def tile_picked_winmax_relu_p_kernel(tc, x_words, x_scales, w1, w2, w3, offs, or
                 nc.scalar.copy(staged[:, ms, :], bank[:])
                 nc.sync.dma_start(out_rows[:, ms, vs], staged[:, ms, :])
 
-        def project_last(c):
+        def project_by_matrix(c, last):
             staged = keep.tile([P, N // P, CHUNK], F32, name="staged%d" % c, align_bytes=64)
             vs = slice(c * CHUNK, (c + 1) * CHUNK)
-            banks = [psum.tile([P, CHUNK], F32, name="res", tag="bank%d" % ((2 * c + m) % 8)) for m in range(N // P)]
+            banks = [psum.tile([P, CHUNK], F32, name="res", tag="bank%d" % m) for m in range(N // P)]
             for u in range(2):
                 for m in range(N // P):
                     one_pass(banks[m][:], c, u, m)
             for m in range(N // P):
-                by_vector = m % 2 == 1
+                by_vector = last and m % 2 == 1
                 (nc.vector.tensor_copy if by_vector else nc.scalar.copy)(staged[:, m, :], banks[m][:])
-                (nc.sync if by_vector else nc.scalar).dma_start(out_rows[:, m : m + 1, vs], staged[:, m : m + 1, :])
+                if last:
+                    (nc.sync if by_vector else nc.scalar).dma_start(out_rows[:, m : m + 1, vs], staged[:, m : m + 1, :])
+                elif m % 2 == 1:
+                    nc.sync.dma_start(out_rows[:, m - 1 : m + 1, vs], staged[:, m - 1 : m + 1, :])
 
         def cast_on_gpsimd(bf, raw_piece):
             nc.gpsimd.tensor_scalar(bf.rearrange("p (c j) -> p c j", j=PACK), raw_piece.rearrange("p j c -> p c j"), 1.0, 0.0, MULT, ADD)
 
-        def quantize_weights(c0, bf):
-            nc.vector.quantize_mx(out=w_codes[:, c0 : c0 + half].bitcast(FP8X4), scales=w_plane[:, c0 : c0 + half], in_=bf)
+        def cast_on_scalar(bf, raw_piece):
+            nc.scalar.copy(bf.rearrange("p (c i j) -> p c j i", i=4, j=PACK), raw_piece.rearrange("p j (c i) -> p c j i", i=4))
 
-        w2_bf = [keep.tile([P, PACK * half], BF16, name="w2_bf%d" % h, tag=("w2_bf0", "w1_codes")[h], align_bytes=64) for h in range(2)]
-        w3_bf = keep.tile([P, PACK * N], BF16, name="w3_bf", tag="w3_bf", align_bytes=64)
+        def quantize_weights(c0, width, bf):
+            nc.vector.quantize_mx(out=w_codes[:, c0 : c0 + width].bitcast(FP8X4), scales=w_plane[:, c0 : c0 + width], in_=bf)
+
+        w2_first = keep.tile([P, PACK * half], BF16, name="w2_first", tag="w2_first", align_bytes=64)
         nc.vector.tensor_copy(
-            w2_bf[0][:].rearrange("p (c i j) -> p c j i", i=4, j=PACK), raw[0].rearrange("p j (c i) -> p c j i", i=4)
+            w2_first[:].rearrange("p (c i j) -> p c j i", i=4, j=PACK), w2_first_raw.rearrange("p j (c i) -> p c j i", i=4)
         )
         early_codes = keep.tile([P, half], U32, name="early_codes", align_bytes=64)
         early_plane = keep.tile([P, half], U8, name="early_plane", align_bytes=64)
-        nc.vector.quantize_mx(out=early_codes[:].bitcast(FP8X4), scales=early_plane[:], in_=w2_bf[0][:])
-        cast_on_gpsimd(w2_bf[1][:, : PACK * piece], raw[1][:, :, :piece])
+        nc.vector.quantize_mx(out=early_codes[:].bitcast(FP8X4), scales=early_plane[:], in_=w2_first[:])
+        w3_bf = keep.tile([P, PACK * N], BF16, name="w3_bf", tag="w3_bf", align_bytes=64)
         for i in range(4):
             cast_on_gpsimd(w3_bf[:, PACK * i * piece : PACK * (i + 1) * piece], w3_raw[:, :, i * piece : (i + 1) * piece])
-        nc.scalar.copy(
-            w2_bf[1][:, PACK * piece :].rearrange("p (c i j) -> p c j i", i=4, j=PACK),
-            raw[1][:, :, piece:].rearrange("p j (c i) -> p c j i", i=4),
-        )
-        gather(0, "looked_up0")
-        weave(0, 2)
-        gather(1, "late")
-        weave(2, 3)
-        weave(3, 4)
-        w_codes = keep.tile([P, 2 * N - half], U32, name="w_codes", tag="looked_up0", align_bytes=64)
+        w2_third = keep.tile([P, PACK * piece], BF16, name="w2_third", tag="w1_codes", align_bytes=64)
+        cast_on_scalar(w2_third[:], w2_third_raw)
+        gather(0, shared.tile([P, PACK, V], BF16, name="looked_up0", offset=0, align_bytes=64))
+        weave(0, 1, "woven0")
+        w2_last = shared.tile([P, PACK * piece], BF16, name="w2_last", offset=0, align_bytes=64)
+        cast_on_scalar(w2_last[:], w2_last_raw)
+        gather(1, keep.tile([P, PACK, V], BF16, name="looked_up1", tag="late", align_bytes=64))
+        weave(1, 2, "picked")
+        w_codes = shared.tile([P, 2 * N - half], U32, name="w_codes", offset=1024, align_bytes=64)
         w_plane = keep.tile([P, 2 * N - half], U8, name="w_plane", align_bytes=64)
         pool_pairs(0, (0,))
-        quantize_weights(0, w2_bf[1][:])
+        quantize_weights(0, piece, w2_third[:])
+        quantize_weights(piece, piece, w2_last[:])
         quantize_pooled(0, 0, 1)
         pool_pairs(0, (1,))
-        quantize_weights(half, w3_bf[:, : PACK * half])
-        quantize_weights(N, w3_bf[:, PACK * half :])
+        quantize_weights(half, half, w3_bf[:, : PACK * half])
+        quantize_weights(N, half, w3_bf[:, PACK * half :])
         quantize_pooled(0, 1, 2)
-        project(0)
-        for c in (1, 2):
-            pool_pairs(c, (0, 1))
-            quantize_pooled(c, 0, 2)
-            project(c)
+        project_by_matrix(0, False)
+        pool_pairs(1, (0, 1))
+        quantize_pooled(1, 0, 2)
+        project_by_tile(1, 4)
+        pool_pairs(2, (0, 1))
+        quantize_pooled(2, 0, 1)
+        quantize_pooled(2, 1, 2)
+        project_by_tile(2, 6)
         pool_pairs(3, (0, 1))
         quantize_pooled(3, 0, 1)
         quantize_pooled(3, 1, 2)
-        project_last(3)
+        project_by_matrix(3, True)

@@ -86,7 +86,7 @@ def tile_picked_winmax_relu_p_kernel(tc, x_words, x_scales, w1, w2, w3, offs, or
                 scales=w1_plane[:, cols],
                 in_=w1_bf[:, t0:t1, :, :].rearrange("p t m j -> p (t m j)"),
             )
-        widths = [(256, 256, 256, 128, 128), (256, 256, 256, 256), (512, 512), (512, 512)]
+        widths = [(256, 256, 256, 128, 128), (256, 256, 256, 256), (512, 256, 256), (512, 512)]
         passes = [(t, sum(w[:i]), sum(w[: i + 1])) for t, w in enumerate(widths) for i in range(len(w))]
         for i, (t, s0, s1) in enumerate(passes):
             cols = slice(t * P, (t + 1) * P)
@@ -212,6 +212,17 @@ def tile_picked_winmax_relu_p_kernel(tc, x_words, x_scales, w1, w2, w3, offs, or
         w_plane = keep.tile([P, 2 * N - half], U8, name="w_plane", align_bytes=64)
         pool_pairs(0, (0,))
         quantize_weights(0, piece, w2_third[:])
+        for bank, width in ((6, 512), (7, 256)):
+            unread = psum.tile([P, width], F32, name="unread", tag="bank%d" % bank)
+            nc.tensor.matmul_mx(
+                out=unread[:],
+                lhsT=w_codes[:, :P].bitcast(FP8X4),
+                lhsT_scale=w_plane[:, :P],
+                rhs=x_codes[:, :width].bitcast(FP8X4),
+                rhs_scale=x_plane[:, :width],
+                start=True,
+                stop=True,
+            )
         quantize_weights(piece, piece, w2_last[:])
         quantize_pooled(0, 0, 1)
         pool_pairs(0, (1,))

@@ -38,12 +38,14 @@ def tile_picked_winmax_relu_p_kernel(tc, x_words, x_scales, w1, w2, w3, offs, or
 
         nc.vector.memset(scale_table[:].bitcast(I32), 0)
         nc.sync.dma_start(offs_sb[:], offs)
-        nc.sync.dma_start(order_sb[:], order)
+        words = x_words[0].rearrange("p c r -> p (c r)").bitcast(I32)
+        nc.sync.dma_start(word_table[:, :256].bitcast(I32), words[:, :256])
         nc.sync.dma_start(scale_table[0:P:8, :].bitcast(I32), x_scales[0].bitcast(I32))
-        nc.sync.dma_start(word_table[:].bitcast(I32), x_words[0].rearrange("p c r -> p (c r)").bitcast(I32))
+        nc.sync.dma_start(word_table[:, 256:].bitcast(I32), words[:, 256:])
         w1_rows = w1.rearrange("(p j) c -> p j c", j=PACK)
         for h in range(2):
             nc.sync.dma_start(w1_raw[h][:], w1_rows[:, :, h * (H // 2) : (h + 1) * (H // 2)])
+        nc.sync.dma_start(order_sb[:], order)
 
         x_plane = keep.tile([P, S], U8, name="x_plane", align_bytes=64)
         nc.vector.memset(x_plane[:].bitcast(I32), 0)
@@ -71,10 +73,15 @@ def tile_picked_winmax_relu_p_kernel(tc, x_words, x_scales, w1, w2, w3, offs, or
         nc.vector.tensor_copy(x_codes[:], word_table[:].indirect(offs_sb[:]))
 
         w1_bf = keep.tile([P, PACK, P, PACK], BF16, name="w1_bf", align_bytes=64)
-        for cast, h, m0, m1 in ((nc.scalar.copy, 0, 0, 64), (nc.scalar.copy, 1, 0, 24), (nc.vector.tensor_copy, 1, 24, 64)):
+        for cast, h, m0, m1, t0, t1 in (
+            (nc.scalar.copy, 0, 0, 64, 0, 4),
+            (nc.scalar.copy, 1, 0, 28, 0, 4),
+            (nc.vector.tensor_copy, 1, 28, 64, 0, 2),
+            (nc.vector.tensor_copy, 1, 28, 64, 2, 4),
+        ):
             cast(
-                w1_bf[:, :, h * (P // 2) + m0 : h * (P // 2) + m1, :].rearrange("p t m j -> p m j t"),
-                w1_raw[h][:].rearrange("p j (m t) -> p m j t", t=PACK)[:, m0:m1],
+                w1_bf[:, t0:t1, h * (P // 2) + m0 : h * (P // 2) + m1, :].rearrange("p t m j -> p m j t"),
+                w1_raw[h][:].rearrange("p j (m t) -> p m j t", t=PACK)[:, m0:m1, :, t0:t1],
             )
         w1_codes = keep.tile([P, H], U32, name="w1_codes", tag="w1_codes", align_bytes=64)
         w1_plane = keep.tile([P, H], U8, name="w1_plane", align_bytes=64)
@@ -154,22 +161,11 @@ def tile_picked_winmax_relu_p_kernel(tc, x_words, x_scales, w1, w2, w3, offs, or
                 stop=(u == 1),
             )
 
-        def project_by_tile(c, bank0):
+        def project(c):
+            last = c == V // CHUNK - 1
             staged = keep.tile([P, N // P, CHUNK], F32, name="staged%d" % c, align_bytes=64)
             vs = slice(c * CHUNK, (c + 1) * CHUNK)
-            for b in range(2):
-                bank = psum.tile([P, 2, CHUNK], F32, name="res", tag="bank%d" % (bank0 + b))
-                for i in range(2):
-                    for u in range(2):
-                        one_pass(bank[:, i, :], c, u, 2 * b + i)
-                ms = slice(2 * b, 2 * b + 2)
-                nc.scalar.copy(staged[:, ms, :], bank[:])
-                nc.sync.dma_start(out_rows[:, ms, vs], staged[:, ms, :])
-
-        def project_by_matrix(c, last):
-            staged = keep.tile([P, N // P, CHUNK], F32, name="staged%d" % c, align_bytes=64)
-            vs = slice(c * CHUNK, (c + 1) * CHUNK)
-            banks = [psum.tile([P, CHUNK], F32, name="res", tag="bank%d" % m) for m in range(N // P)]
+            banks = [psum.tile([P, CHUNK], F32, name="res", tag="bank%d" % (4 * (c % 2) + m)) for m in range(N // P)]
             for u in range(2):
                 for m in range(N // P):
                     one_pass(banks[m][:], c, u, m)
@@ -178,6 +174,9 @@ def tile_picked_winmax_relu_p_kernel(tc, x_words, x_scales, w1, w2, w3, offs, or
                 (nc.vector.tensor_copy if by_vector else nc.scalar.copy)(staged[:, m, :], banks[m][:])
                 if last:
                     (nc.sync if by_vector else nc.scalar).dma_start(out_rows[:, m : m + 1, vs], staged[:, m : m + 1, :])
+                elif c == 1:
+                    if m == N // P - 1:
+                        nc.sync.dma_start(out_rows[:, :, vs], staged[:])
                 elif m % 2 == 1:
                     nc.sync.dma_start(out_rows[:, m - 1 : m + 1, vs], staged[:, m - 1 : m + 1, :])
 
@@ -212,7 +211,7 @@ def tile_picked_winmax_relu_p_kernel(tc, x_words, x_scales, w1, w2, w3, offs, or
         w_plane = keep.tile([P, 2 * N - half], U8, name="w_plane", align_bytes=64)
         pool_pairs(0, (0,))
         quantize_weights(0, piece, w2_third[:])
-        for bank, width in ((6, 512), (7, 256)):
+        for bank, width in ((4, 512), (5, 256)):
             unread = psum.tile([P, width], F32, name="unread", tag="bank%d" % bank)
             nc.tensor.matmul_mx(
                 out=unread[:],
@@ -229,15 +228,9 @@ def tile_picked_winmax_relu_p_kernel(tc, x_words, x_scales, w1, w2, w3, offs, or
         quantize_weights(half, half, w3_bf[:, : PACK * half])
         quantize_weights(N, half, w3_bf[:, PACK * half :])
         quantize_pooled(0, 1, 2)
-        project_by_matrix(0, False)
-        pool_pairs(1, (0, 1))
-        quantize_pooled(1, 0, 2)
-        project_by_tile(1, 4)
-        pool_pairs(2, (0, 1))
-        quantize_pooled(2, 0, 1)
-        quantize_pooled(2, 1, 2)
-        project_by_tile(2, 6)
-        pool_pairs(3, (0, 1))
-        quantize_pooled(3, 0, 1)
-        quantize_pooled(3, 1, 2)
-        project_by_matrix(3, True)
+        project(0)
+        for c in range(1, V // CHUNK):
+            pool_pairs(c, (0, 1))
+            quantize_pooled(c, 0, 1)
+            quantize_pooled(c, 1, 2)
+            project(c)

@@ -13,6 +13,7 @@ U16 = mybir.dt.uint16
 U8 = mybir.dt.uint8
 FP8X4 = mybir.dt.float8_e4m3fn_x4
 RELU = mybir.ActivationFunctionType.Relu
+COPY = mybir.ActivationFunctionType.Copy
 MAX = mybir.AluOpType.max
 MIN = mybir.AluOpType.min
 MULT = mybir.AluOpType.mult
@@ -21,6 +22,7 @@ ADD = mybir.AluOpType.add
 P = 128
 PACK = 4
 CHUNK = 128
+PIECE = 256
 
 
 def tile_picked_winmax_relu_p_kernel(tc, x_words, x_scales, w1, w2, w3, offs, order, out):
@@ -32,205 +34,170 @@ def tile_picked_winmax_relu_p_kernel(tc, x_words, x_scales, w1, w2, w3, offs, or
 
         offs_sb = keep.tile([P, S // 16], U16, name="offs_sb")
         order_sb = keep.tile([P, S // 16], U16, name="order_sb")
-        scale_table = keep.tile([P, T], U8, name="scale_table", tag="late", align_bytes=64)
+        scale_table = keep.tile([P, T], U8, name="scale_table", align_bytes=64)
         word_table = keep.tile([P, T], U32, name="word_table", align_bytes=64)
         w1_raw = [keep.tile([P, PACK, H // 2], F32, name="w1_raw%d" % h, align_bytes=64) for h in range(2)]
 
         nc.vector.memset(scale_table[:].bitcast(I32), 0)
         nc.sync.dma_start(offs_sb[:], offs)
-        words = x_words[0].rearrange("p c r -> p (c r)").bitcast(I32)
-        nc.sync.dma_start(word_table[:, :256].bitcast(I32), words[:, :256])
-        nc.sync.dma_start(scale_table[0:P:8, :].bitcast(I32), x_scales[0].bitcast(I32))
-        nc.sync.dma_start(word_table[:, 256:].bitcast(I32), words[:, 256:])
-        w1_rows = w1.rearrange("(p j) c -> p j c", j=PACK)
-        for h in range(2):
-            nc.sync.dma_start(w1_raw[h][:], w1_rows[:, :, h * (H // 2) : (h + 1) * (H // 2)])
         nc.sync.dma_start(order_sb[:], order)
+        for e in range(2):
+            nc.sync.dma_start(scale_table[e:P:16, :].bitcast(I32), x_scales[0].bitcast(I32)[e::2, :])
+        for h in range(2):
+            nc.sync.dma_start(w1_raw[h][:], w1.rearrange("(p j) c -> p j c", j=PACK)[:, :, h * H // 2 : (h + 1) * H // 2])
+        nc.sync.dma_start(word_table[:].bitcast(I32), x_words[0].rearrange("p c r -> p (c r)").bitcast(I32))
 
-        x_plane = keep.tile([P, S], U8, name="x_plane", align_bytes=64)
-        nc.vector.memset(x_plane[:].bitcast(I32), 0)
-        picked_scales = keep.tile([P, S], U8, name="picked_scales", tag="picked", align_bytes=64)
-        nc.vector.tensor_copy(picked_scales[:], scale_table[:].indirect(offs_sb[:]))
-        for q in range(4):
-            nc.sync.dma_start(
-                x_plane[32 * q : 32 * q + 4, :].bitcast(I32),
-                picked_scales[32 * q : 32 * q + 32 : 8, :].bitcast(I32),
-            )
-        w_rows = [w.rearrange("(p j) c -> p j c", j=PACK) for w in (w2, w3)]
-        half, piece = N // 2, N // 4
-        w2_raw = keep.tile([P, PACK * 3 * piece], F32, name="w2_raw", tag="late", align_bytes=64)
-        w2_first_raw = w2_raw[:, : PACK * half].rearrange("p (j c) -> p j c", j=PACK)
-        w2_third_raw = w2_raw[:, PACK * half :].rearrange("p (j c) -> p j c", j=PACK)
-        nc.sync.dma_start(w2_first_raw, w_rows[0][:, :, :half])
-        nc.sync.dma_start(w2_third_raw, w_rows[0][:, :, half : 3 * piece])
-        last_raw = keep.tile([P, PACK * (N + piece)], F32, name="last_raw", tag="picked", align_bytes=64)
-        w3_raw = last_raw[:, : PACK * N].rearrange("p (j c) -> p j c", j=PACK)
-        w2_last_raw = last_raw[:, PACK * N :].rearrange("p (j c) -> p j c", j=PACK)
-        nc.sync.dma_start(w3_raw, w_rows[1])
-        nc.sync.dma_start(w2_last_raw, w_rows[0][:, :, 3 * piece :])
+        half = N // 2
+        raw_first = shared.tile([P, PACK * half], F32, name="raw_first", offset=0, align_bytes=64)
+        raw_rest = shared.tile([P, 3 * PACK * half], F32, name="raw_rest", offset=4352, align_bytes=64)
+        raw_halves = [raw_first[:].rearrange("p (j c) -> p j c", j=PACK)]
+        raw_halves += [raw_rest[:, i * PACK * half : (i + 1) * PACK * half].rearrange("p (j c) -> p j c", j=PACK) for i in range(3)]
 
-        x_codes = keep.tile([P, S], U32, name="x_codes", align_bytes=64)
-        nc.vector.tensor_copy(x_codes[:], word_table[:].indirect(offs_sb[:]))
+        def load_weights(i):
+            rows = (w2, w3)[i // 2].rearrange("(p j) c -> p j c", j=PACK)
+            nc.sync.dma_start(raw_halves[i], rows[:, :, i % 2 * half : (i % 2 + 1) * half])
 
-        w1_bf = keep.tile([P, PACK, P, PACK], BF16, name="w1_bf", align_bytes=64)
-        for cast, h, m0, m1, t0, t1 in (
-            (nc.scalar.copy, 0, 0, 64, 0, 4),
-            (nc.scalar.copy, 1, 0, 28, 0, 4),
-            (nc.vector.tensor_copy, 1, 28, 64, 0, 2),
-            (nc.vector.tensor_copy, 1, 28, 64, 2, 4),
-        ):
-            cast(
-                w1_bf[:, t0:t1, h * (P // 2) + m0 : h * (P // 2) + m1, :].rearrange("p t m j -> p m j t"),
-                w1_raw[h][:].rearrange("p j (m t) -> p m j t", t=PACK)[:, m0:m1, :, t0:t1],
-            )
+        x_planes = []
+        for h in range(2):
+            picked = shared.tile([P, S // 2], U8, name="picked%d" % h, offset=3840 + 256 * h, align_bytes=64)
+            plane = keep.tile([P, S // 2], U8, name="x_plane%d" % h, align_bytes=64)
+            nc.vector.tensor_copy(picked[:], scale_table[:].indirect(offs_sb[:, h * S // 32 : (h + 1) * S // 32]))
+            nc.vector.tensor_copy(plane[:].bitcast(I32), picked[:].bitcast(I32))
+            for e in range(2):
+                nc.sync.dma_start(plane[2 + e : P : 32, :].bitcast(I32), plane[16 + e : P : 32, :].bitcast(I32))
+            x_planes.append(plane)
+            if h == 0:
+                load_weights(0)
+        for i in range(1, 4):
+            load_weights(i)
+
         w1_codes = keep.tile([P, H], U32, name="w1_codes", tag="w1_codes", align_bytes=64)
         w1_plane = keep.tile([P, H], U8, name="w1_plane", align_bytes=64)
-        y = [keep.tile([P, S], F32, name="y%d" % t, align_bytes=64) for t in range(PACK)]
-        for t0, t1 in ((0, 1), (1, 2), (2, 4)):
-            cols = slice(t0 * P, t1 * P)
-            nc.vector.quantize_mx(
-                out=w1_codes[:, cols].bitcast(FP8X4),
-                scales=w1_plane[:, cols],
-                in_=w1_bf[:, t0:t1, :, :].rearrange("p t m j -> p (t m j)"),
+        for h in range(2):
+            w1_bf = keep.tile([P, PACK, P // 2, PACK], BF16, name="w1_bf%d" % h, tag=("w1_bf0", "x_codes")[h], align_bytes=64)
+            nc.scalar.copy(w1_bf[:].rearrange("p t m j -> p m j t"), w1_raw[h][:].rearrange("p j (m t) -> p m j t", t=PACK))
+            for t in range(PACK):
+                cols = slice(t * P + h * P // 2, t * P + (h + 1) * P // 2)
+                nc.vector.quantize_mx(
+                    out=w1_codes[:, cols].bitcast(FP8X4), scales=w1_plane[:, cols], in_=w1_bf[:, t].rearrange("p m j -> p (m j)")
+                )
+
+        x_codes = keep.tile([P, S], U32, name="x_codes", tag="x_codes", align_bytes=64)
+        for s0 in range(0, S, PIECE):
+            nc.vector.tensor_copy(x_codes[:, s0 : s0 + PIECE], word_table[:].indirect(offs_sb[:, s0 // 16 : (s0 + PIECE) // 16]))
+
+        w_bf = keep.tile([P, 2 * PACK * N], BF16, name="w_bf", tag="w_bf", align_bytes=64)
+        for i, view in enumerate(raw_halves):
+            nc.gpsimd.tensor_scalar(
+                w_bf[:, i * PACK * half : (i + 1) * PACK * half].rearrange("p (c j) -> p c j", j=PACK),
+                view.rearrange("p j c -> p c j"),
+                1.0,
+                0.0,
+                MULT,
+                ADD,
             )
-        widths = [(256, 256, 256, 128, 128), (256, 256, 256, 256), (512, 256, 256), (512, 512)]
-        passes = [(t, sum(w[:i]), sum(w[: i + 1])) for t, w in enumerate(widths) for i in range(len(w))]
-        for i, (t, s0, s1) in enumerate(passes):
+
+        y = [keep.tile([P, S], F32, name="y%d" % t, align_bytes=64) for t in range(PACK)]
+        passes = [(t, a, a + 1) for a in range(4) for t in range(2)] + [(t, a, a + 2) for t in (2, 3) for a in (0, 2)]
+        for i, (t, a, b) in enumerate(passes):
             cols = slice(t * P, (t + 1) * P)
-            acc = psum.tile([P, s1 - s0], F32, name="acc", tag="bank%d" % (i % 8))
+            s0, s1 = a * PIECE, b * PIECE
+            acc = psum.tile([P, s1 - s0], F32, name="acc", tag="bank%d" % (i if i < 8 else (4, 0, 5, 1)[i - 8]))
             nc.tensor.matmul_mx(
                 out=acc[:],
                 lhsT=w1_codes[:, cols].bitcast(FP8X4),
                 lhsT_scale=w1_plane[:, cols],
                 rhs=x_codes[:, s0:s1].bitcast(FP8X4),
-                rhs_scale=x_plane[:, s0:s1],
+                rhs_scale=x_planes[a // 2][:, s0 % (S // 2) : s0 % (S // 2) + s1 - s0],
                 start=True,
                 stop=True,
             )
-            if i == 2:
+            if (t, a) == (1, 2):
                 nc.vector.tensor_scalar_max(y[t][:, s0:s1], acc[:], 0.0)
             else:
                 nc.scalar.activation(y[t][:, s0:s1], acc[:], RELU)
 
-        out_rows = out.rearrange("(m p) v -> p m v", p=P)
-        looked_up, woven, z_bf, z_codes, z_plane = {}, {}, {}, {}, {}
+        def gather(planes, t, e0, e1):
+            looked_up = y[t][:].indirect(order_sb[:, e0 // 16 : e1 // 16])
+            if e0 == 0 and t < PACK - 1:
+                nc.vector.tensor_copy(planes[:, t, :], looked_up)
+            else:
+                nc.scalar.activation(planes[:, t, :], looked_up, COPY)
 
-        def gather(h, planes):
-            looked_up[h] = planes
+        first = keep.tile([P, PACK, 2 * PIECE], BF16, name="first", align_bytes=64)
+        third = keep.tile([P, PACK, PIECE], BF16, name="third", tag="x_codes", align_bytes=64)
+        fourth = keep.tile([P, PACK, PIECE], BF16, name="fourth", tag="w1_codes", align_bytes=64)
+        for planes, e0, e1 in ((first, 0, 2 * PIECE), (third, 2 * PIECE, 3 * PIECE), (fourth, 3 * PIECE, 4 * PIECE)):
             for t in range(PACK):
-                nc.vector.tensor_copy(looked_up[h][:, t, :], y[t][:].indirect(order_sb[:, h * V // 16 : (h + 1) * V // 16]))
+                gather(planes, t, e0, e1)
+        pairs = [first[:, :, :PIECE], first[:, :, PIECE:], third[:], fourth[:]]
 
-        def weave(h, parts, tag):
-            tile = keep.tile([P, parts, 2, V * PACK // (2 * parts)], BF16, name="woven%d" % h, tag=tag, align_bytes=64)
-            for part in range(parts):
-                nc.scalar.copy(
-                    tile[:, part].rearrange("p s (c i t) -> p c t i s", i=2, t=PACK),
-                    looked_up[h][:, :, part * V // parts : (part + 1) * V // parts].rearrange("p t (c i s) -> p c t i s", i=2, s=2),
-                )
-            for i in range(2):
-                woven[2 * h + i] = tile[:, i] if parts == 2 else tile[:, 0, :, i * CHUNK * PACK : (i + 1) * CHUNK * PACK]
+        w_codes = keep.tile([P, 2 * N], U32, name="w_codes", align_bytes=64)
+        w_plane = keep.tile([P, 2 * N], U8, name="w_plane", align_bytes=64)
+        nc.vector.quantize_mx(out=w_codes[:].bitcast(FP8X4), scales=w_plane[:], in_=w_bf[:])
 
-        def pool_pairs(c, which):
-            if c not in z_bf:
-                z_bf[c] = keep.tile([P, 2, CHUNK * PACK], BF16, name="z_bf%d" % c, tag=("z_bf0", "w3_bf", "z_bf0", "z_bf3")[c], align_bytes=64)
-            for u in which:
-                nc.vector.tensor_tensor(z_bf[c][:, u, :], woven[c][:, 0, :], woven[c][:, 1, :], (MAX, MIN)[u])
+        z_bf = keep.tile([P, 2 * V * PACK], BF16, name="z_bf", tag="w_bf", align_bytes=64)
+        z_codes = keep.tile([P, 2 * V], U32, name="z_codes", align_bytes=64)
+        z_plane = keep.tile([P, 2 * V], U8, name="z_plane", align_bytes=64)
+        out_rows = out.rearrange("(m p) v -> p m v", p=P)
 
-        def quantize_pooled(c, u0, u1):
-            if c not in z_codes:
-                z_codes[c] = keep.tile([P, 2 * CHUNK], U32, name="z_codes%d" % c, align_bytes=64)
-                z_plane[c] = keep.tile([P, 2 * CHUNK], U8, name="z_plane%d" % c, align_bytes=64)
-            cols = slice(u0 * CHUNK, u1 * CHUNK)
-            nc.vector.quantize_mx(
-                out=z_codes[c][:, cols].bitcast(FP8X4),
-                scales=z_plane[c][:, cols],
-                in_=z_bf[c][:, u0:u1, :].rearrange("p u e -> p (u e)"),
+        def pool_pairs(c, u):
+            members = pairs[c].rearrange("p t (g i s) -> p g t i s", i=2, s=2)
+            z0 = (2 * c + u) * CHUNK * PACK
+            nc.vector.tensor_tensor(
+                z_bf[:, z0 : z0 + CHUNK * PACK].rearrange("p (g i t) -> p g t i", i=2, t=PACK),
+                members[:, :, :, :, 0],
+                members[:, :, :, :, 1],
+                (MAX, MIN)[u],
             )
 
+        def quantize_pooled(c, u0, u1):
+            c0, c1 = (2 * c + u0) * CHUNK, (2 * c + u1) * CHUNK
+            nc.vector.quantize_mx(out=z_codes[:, c0:c1].bitcast(FP8X4), scales=z_plane[:, c0:c1], in_=z_bf[:, PACK * c0 : PACK * c1])
+
         def one_pass(res, c, u, m):
-            codes, plane, c0 = (early_codes, early_plane, 0) if u * N + m * P < half else (w_codes, w_plane, half)
-            w_cols = slice(u * N + m * P - c0, u * N + (m + 1) * P - c0)
-            z_cols = slice(u * CHUNK, (u + 1) * CHUNK)
+            w_cols = slice(u * N + m * P, u * N + (m + 1) * P)
+            z_cols = slice((2 * c + u) * CHUNK, (2 * c + u + 1) * CHUNK)
             nc.tensor.matmul_mx(
                 out=res,
-                lhsT=codes[:, w_cols].bitcast(FP8X4),
-                lhsT_scale=plane[:, w_cols],
-                rhs=z_codes[c][:, z_cols].bitcast(FP8X4),
-                rhs_scale=z_plane[c][:, z_cols],
+                lhsT=w_codes[:, w_cols].bitcast(FP8X4),
+                lhsT_scale=w_plane[:, w_cols],
+                rhs=z_codes[:, z_cols].bitcast(FP8X4),
+                rhs_scale=z_plane[:, z_cols],
                 start=(u == 0),
                 stop=(u == 1),
             )
 
         def project(c):
-            last = c == V // CHUNK - 1
             staged = keep.tile([P, N // P, CHUNK], F32, name="staged%d" % c, align_bytes=64)
-            vs = slice(c * CHUNK, (c + 1) * CHUNK)
-            banks = [psum.tile([P, CHUNK], F32, name="res", tag="bank%d" % (4 * (c % 2) + m)) for m in range(N // P)]
+            bank = psum.tile([P, N // P, CHUNK], F32, name="res", tag="bank%d" % c)
+            for m in range(N // P):
+                for u in range(2):
+                    one_pass(bank[:, m, :], c, u, m)
+            nc.scalar.copy(staged[:], bank[:])
+            nc.sync.dma_start(out_rows[:, :, c * CHUNK : (c + 1) * CHUNK], staged[:])
+
+        def project_last(c):
+            staged = keep.tile([P, N // P, CHUNK], F32, name="staged%d" % c, align_bytes=64)
+            banks = [psum.tile([P, CHUNK], F32, name="res", tag="bank%d" % (4 + m)) for m in range(N // P)]
             for u in range(2):
                 for m in range(N // P):
                     one_pass(banks[m][:], c, u, m)
             for m in range(N // P):
-                by_vector = last and m % 2 == 1
+                by_vector = m % 2 == 1
                 (nc.vector.tensor_copy if by_vector else nc.scalar.copy)(staged[:, m, :], banks[m][:])
-                if last:
-                    (nc.sync if by_vector else nc.scalar).dma_start(out_rows[:, m : m + 1, vs], staged[:, m : m + 1, :])
-                elif c == 1:
-                    if m == N // P - 1:
-                        nc.sync.dma_start(out_rows[:, :, vs], staged[:])
-                elif m % 2 == 1:
-                    nc.sync.dma_start(out_rows[:, m - 1 : m + 1, vs], staged[:, m - 1 : m + 1, :])
+                (nc.sync if by_vector else nc.scalar).dma_start(
+                    out_rows[:, m : m + 1, c * CHUNK : (c + 1) * CHUNK], staged[:, m : m + 1, :]
+                )
 
-        def cast_on_gpsimd(bf, raw_piece):
-            nc.gpsimd.tensor_scalar(bf.rearrange("p (c j) -> p c j", j=PACK), raw_piece.rearrange("p j c -> p c j"), 1.0, 0.0, MULT, ADD)
-
-        def cast_on_scalar(bf, raw_piece):
-            nc.scalar.copy(bf.rearrange("p (c i j) -> p c j i", i=4, j=PACK), raw_piece.rearrange("p j (c i) -> p c j i", i=4))
-
-        def quantize_weights(c0, width, bf):
-            nc.vector.quantize_mx(out=w_codes[:, c0 : c0 + width].bitcast(FP8X4), scales=w_plane[:, c0 : c0 + width], in_=bf)
-
-        w2_first = keep.tile([P, PACK * half], BF16, name="w2_first", tag="w2_first", align_bytes=64)
-        nc.vector.tensor_copy(
-            w2_first[:].rearrange("p (c i j) -> p c j i", i=4, j=PACK), w2_first_raw.rearrange("p j (c i) -> p c j i", i=4)
-        )
-        early_codes = keep.tile([P, half], U32, name="early_codes", align_bytes=64)
-        early_plane = keep.tile([P, half], U8, name="early_plane", align_bytes=64)
-        nc.vector.quantize_mx(out=early_codes[:].bitcast(FP8X4), scales=early_plane[:], in_=w2_first[:])
-        w3_bf = keep.tile([P, PACK * N], BF16, name="w3_bf", tag="w3_bf", align_bytes=64)
-        for i in range(4):
-            cast_on_gpsimd(w3_bf[:, PACK * i * piece : PACK * (i + 1) * piece], w3_raw[:, :, i * piece : (i + 1) * piece])
-        w2_third = keep.tile([P, PACK * piece], BF16, name="w2_third", tag="w1_codes", align_bytes=64)
-        cast_on_scalar(w2_third[:], w2_third_raw)
-        gather(0, shared.tile([P, PACK, V], BF16, name="looked_up0", offset=0, align_bytes=64))
-        weave(0, 1, "woven0")
-        w2_last = shared.tile([P, PACK * piece], BF16, name="w2_last", offset=0, align_bytes=64)
-        cast_on_scalar(w2_last[:], w2_last_raw)
-        gather(1, keep.tile([P, PACK, V], BF16, name="looked_up1", tag="late", align_bytes=64))
-        weave(1, 2, "picked")
-        w_codes = shared.tile([P, 2 * N - half], U32, name="w_codes", offset=1024, align_bytes=64)
-        w_plane = keep.tile([P, 2 * N - half], U8, name="w_plane", align_bytes=64)
-        pool_pairs(0, (0,))
-        quantize_weights(0, piece, w2_third[:])
-        for bank, width in ((4, 512), (5, 256)):
-            unread = psum.tile([P, width], F32, name="unread", tag="bank%d" % bank)
-            nc.tensor.matmul_mx(
-                out=unread[:],
-                lhsT=w_codes[:, :P].bitcast(FP8X4),
-                lhsT_scale=w_plane[:, :P],
-                rhs=x_codes[:, :width].bitcast(FP8X4),
-                rhs_scale=x_plane[:, :width],
-                start=True,
-                stop=True,
-            )
-        quantize_weights(piece, piece, w2_last[:])
-        quantize_pooled(0, 0, 1)
-        pool_pairs(0, (1,))
-        quantize_weights(half, half, w3_bf[:, : PACK * half])
-        quantize_weights(N, half, w3_bf[:, PACK * half :])
-        quantize_pooled(0, 1, 2)
-        project(0)
-        for c in range(1, V // CHUNK):
-            pool_pairs(c, (0, 1))
-            quantize_pooled(c, 0, 1)
-            quantize_pooled(c, 1, 2)
+        last = V // CHUNK - 1
+        pool_pairs(0, 0)
+        for c in range(last):
+            pool_pairs(c, 1)
+            pool_pairs(c + 1, 0)
+            quantize_pooled(c, 0, 2)
             project(c)
+        pool_pairs(last, 1)
+        quantize_pooled(last, 0, 1)
+        quantize_pooled(last, 1, 2)
+        project_last(last)

@@ -34,88 +34,106 @@ def tile_picked_winmax_relu_p_kernel(tc, x_words, x_scales, w1, w2, w3, offs, or
 
         offs_sb = keep.tile([P, S // 16], U16, name="offs_sb")
         order_sb = keep.tile([P, S // 16], U16, name="order_sb")
-        scale_table = keep.tile([P, T], U8, name="scale_table", align_bytes=64)
+        scale_table = keep.tile([P, T], U8, name="scale_table", tag="late", align_bytes=64)
         word_table = keep.tile([P, T], U32, name="word_table", align_bytes=64)
         w1_raw = [keep.tile([P, PACK, H // 2], F32, name="w1_raw%d" % h, align_bytes=64) for h in range(2)]
 
         nc.vector.memset(scale_table[:].bitcast(I32), 0)
         nc.sync.dma_start(offs_sb[:], offs)
+        words = x_words[0].rearrange("p c r -> p (c r)").bitcast(I32)
+        nc.sync.dma_start(word_table[:, :256].bitcast(I32), words[:, :256])
+        nc.sync.dma_start(scale_table[0:P:8, :].bitcast(I32), x_scales[0].bitcast(I32))
+        nc.sync.dma_start(word_table[:, 256:].bitcast(I32), words[:, 256:])
+        w1_rows = w1.rearrange("(p j) c -> p j c", j=PACK)
+        for h in range(2):
+            nc.sync.dma_start(w1_raw[h][:], w1_rows[:, :, h * (H // 2) : (h + 1) * (H // 2)])
         nc.sync.dma_start(order_sb[:], order)
-        for e in range(2):
-            nc.sync.dma_start(scale_table[e:P:16, :].bitcast(I32), x_scales[0].bitcast(I32)[e::2, :])
-        for h in range(2):
-            nc.sync.dma_start(w1_raw[h][:], w1.rearrange("(p j) c -> p j c", j=PACK)[:, :, h * H // 2 : (h + 1) * H // 2])
-        nc.sync.dma_start(word_table[:].bitcast(I32), x_words[0].rearrange("p c r -> p (c r)").bitcast(I32))
 
+        x_plane = keep.tile([P, S], U8, name="x_plane", align_bytes=64)
+        nc.vector.memset(x_plane[:].bitcast(I32), 0)
+        picked_scales = keep.tile([P, S], U8, name="picked_scales", tag="picked", align_bytes=64)
+        nc.vector.tensor_copy(picked_scales[:], scale_table[:].indirect(offs_sb[:]))
+        for q in range(4):
+            nc.sync.dma_start(
+                x_plane[32 * q : 32 * q + 4, :].bitcast(I32),
+                picked_scales[32 * q : 32 * q + 32 : 8, :].bitcast(I32),
+            )
         half = N // 2
-        raw_first = shared.tile([P, PACK * half], F32, name="raw_first", offset=0, align_bytes=64)
-        raw_rest = shared.tile([P, 3 * PACK * half], F32, name="raw_rest", offset=4352, align_bytes=64)
-        raw_halves = [raw_first[:].rearrange("p (j c) -> p j c", j=PACK)]
-        raw_halves += [raw_rest[:, i * PACK * half : (i + 1) * PACK * half].rearrange("p (j c) -> p j c", j=PACK) for i in range(3)]
-
-        def load_weights(i):
-            rows = (w2, w3)[i // 2].rearrange("(p j) c -> p j c", j=PACK)
-            nc.sync.dma_start(raw_halves[i], rows[:, :, i % 2 * half : (i % 2 + 1) * half])
-
-        x_planes = []
-        for h in range(2):
-            picked = shared.tile([P, S // 2], U8, name="picked%d" % h, offset=3840 + 256 * h, align_bytes=64)
-            plane = keep.tile([P, S // 2], U8, name="x_plane%d" % h, align_bytes=64)
-            nc.vector.tensor_copy(picked[:], scale_table[:].indirect(offs_sb[:, h * S // 32 : (h + 1) * S // 32]))
-            nc.vector.tensor_copy(plane[:].bitcast(I32), picked[:].bitcast(I32))
-            for e in range(2):
-                nc.sync.dma_start(plane[2 + e : P : 32, :].bitcast(I32), plane[16 + e : P : 32, :].bitcast(I32))
-            x_planes.append(plane)
-            if h == 0:
-                load_weights(0)
-        for i in range(1, 4):
-            load_weights(i)
-
-        w1_codes = keep.tile([P, H], U32, name="w1_codes", tag="w1_codes", align_bytes=64)
-        w1_plane = keep.tile([P, H], U8, name="w1_plane", align_bytes=64)
-        for h in range(2):
-            w1_bf = keep.tile([P, PACK, P // 2, PACK], BF16, name="w1_bf%d" % h, tag=("w1_bf0", "x_codes")[h], align_bytes=64)
-            nc.scalar.copy(w1_bf[:].rearrange("p t m j -> p m j t"), w1_raw[h][:].rearrange("p j (m t) -> p m j t", t=PACK))
-            for t in range(PACK):
-                cols = slice(t * P + h * P // 2, t * P + (h + 1) * P // 2)
-                nc.vector.quantize_mx(
-                    out=w1_codes[:, cols].bitcast(FP8X4), scales=w1_plane[:, cols], in_=w1_bf[:, t].rearrange("p m j -> p (m j)")
-                )
+        raw_halves = []
+        for w, tag in ((w2, "late"), (w3, "picked")):
+            raw = keep.tile([P, PACK * N], F32, name="raw_" + tag, tag=tag, align_bytes=64)
+            rows = w.rearrange("(p j) c -> p j c", j=PACK)
+            for h in range(2):
+                view = raw[:, h * PACK * half : (h + 1) * PACK * half].rearrange("p (j c) -> p j c", j=PACK)
+                nc.sync.dma_start(view, rows[:, :, h * half : (h + 1) * half])
+                raw_halves.append(view)
 
         x_codes = keep.tile([P, S], U32, name="x_codes", tag="x_codes", align_bytes=64)
-        for s0 in range(0, S, PIECE):
-            nc.vector.tensor_copy(x_codes[:, s0 : s0 + PIECE], word_table[:].indirect(offs_sb[:, s0 // 16 : (s0 + PIECE) // 16]))
+        nc.vector.tensor_copy(x_codes[:], word_table[:].indirect(offs_sb[:]))
 
-        w_bf = keep.tile([P, 2 * PACK * N], BF16, name="w_bf", tag="w_bf", align_bytes=64)
-        for i, view in enumerate(raw_halves):
-            nc.gpsimd.tensor_scalar(
-                w_bf[:, i * PACK * half : (i + 1) * PACK * half].rearrange("p (c j) -> p c j", j=PACK),
-                view.rearrange("p j c -> p c j"),
-                1.0,
-                0.0,
-                MULT,
-                ADD,
+        w1_bf = keep.tile([P, PACK, P, PACK], BF16, name="w1_bf", align_bytes=64)
+        for cast, h, m0, m1, t0, t1 in (
+            (nc.scalar.copy, 0, 0, 64, 0, 4),
+            (nc.scalar.copy, 1, 0, 28, 0, 4),
+            (nc.vector.tensor_copy, 1, 28, 64, 0, 2),
+            (nc.vector.tensor_copy, 1, 28, 64, 2, 4),
+        ):
+            cast(
+                w1_bf[:, t0:t1, h * (P // 2) + m0 : h * (P // 2) + m1, :].rearrange("p t m j -> p m j t"),
+                w1_raw[h][:].rearrange("p j (m t) -> p m j t", t=PACK)[:, m0:m1, :, t0:t1],
             )
-
+        w1_codes = keep.tile([P, H], U32, name="w1_codes", tag="w1_codes", align_bytes=64)
+        w1_plane = keep.tile([P, H], U8, name="w1_plane", align_bytes=64)
         y = [keep.tile([P, S], F32, name="y%d" % t, align_bytes=64) for t in range(PACK)]
-        passes = [(t, a, a + 1) for a in range(4) for t in range(2)] + [(t, a, a + 2) for t in (2, 3) for a in (0, 2)]
-        for i, (t, a, b) in enumerate(passes):
+        for t0, t1 in ((0, 1), (1, 2), (2, 4)):
+            cols = slice(t0 * P, t1 * P)
+            nc.vector.quantize_mx(
+                out=w1_codes[:, cols].bitcast(FP8X4),
+                scales=w1_plane[:, cols],
+                in_=w1_bf[:, t0:t1, :, :].rearrange("p t m j -> p (t m j)"),
+            )
+        widths = [(256, 256, 256, 128, 128), (512, 512), (512, 512), (512, 512)]
+        passes = [(t, sum(w[:i]), sum(w[: i + 1])) for t, w in enumerate(widths) for i in range(len(w))]
+        for i, (t, s0, s1) in enumerate(passes):
             cols = slice(t * P, (t + 1) * P)
-            s0, s1 = a * PIECE, b * PIECE
-            acc = psum.tile([P, s1 - s0], F32, name="acc", tag="bank%d" % (i if i < 8 else (4, 0, 5, 1)[i - 8]))
+            acc = psum.tile([P, s1 - s0], F32, name="acc", tag="bank%d" % (i % 8))
             nc.tensor.matmul_mx(
                 out=acc[:],
                 lhsT=w1_codes[:, cols].bitcast(FP8X4),
                 lhsT_scale=w1_plane[:, cols],
                 rhs=x_codes[:, s0:s1].bitcast(FP8X4),
-                rhs_scale=x_planes[a // 2][:, s0 % (S // 2) : s0 % (S // 2) + s1 - s0],
+                rhs_scale=x_plane[:, s0:s1],
                 start=True,
                 stop=True,
             )
-            if (t, a) == (1, 2):
+            if i == len(passes) - 1:
                 nc.vector.tensor_scalar_max(y[t][:, s0:s1], acc[:], 0.0)
             else:
                 nc.scalar.activation(y[t][:, s0:s1], acc[:], RELU)
+
+        early_codes = keep.tile([P, half], U32, name="early_codes", align_bytes=64)
+        early_plane = keep.tile([P, half], U8, name="early_plane", align_bytes=64)
+        early_bf = shared.tile([P, PACK * half], BF16, name="early_bf", offset=3072, align_bytes=64)
+        for m in range(2):
+            nc.vector.tensor_copy(
+                early_bf[:, m * PACK * P : (m + 1) * PACK * P].rearrange("p (c i j) -> p c j i", i=4, j=PACK),
+                raw_halves[0][:, :, m * P : (m + 1) * P].rearrange("p j (c i) -> p c j i", i=4),
+            )
+        for m in range(2):
+            cols = slice(m * P, (m + 1) * P)
+            nc.vector.quantize_mx(
+                out=early_codes[:, cols].bitcast(FP8X4), scales=early_plane[:, cols], in_=early_bf[:, m * PACK * P : (m + 1) * PACK * P]
+            )
+        w_bf = shared.tile([P, 3 * PACK * half], BF16, name="w_bf", offset=4096, align_bytes=64)
+        for i in range(3):
+            nc.gpsimd.tensor_scalar(
+                w_bf[:, i * PACK * half : (i + 1) * PACK * half].rearrange("p (c j) -> p c j", j=PACK),
+                raw_halves[i + 1].rearrange("p j c -> p c j"),
+                1.0,
+                0.0,
+                MULT,
+                ADD,
+            )
 
         def gather(planes, t, e0, e1):
             looked_up = y[t][:].indirect(order_sb[:, e0 // 16 : e1 // 16])
@@ -124,7 +142,7 @@ def tile_picked_winmax_relu_p_kernel(tc, x_words, x_scales, w1, w2, w3, offs, or
             else:
                 nc.scalar.activation(planes[:, t, :], looked_up, COPY)
 
-        first = keep.tile([P, PACK, 2 * PIECE], BF16, name="first", align_bytes=64)
+        first = shared.tile([P, PACK, 2 * PIECE], BF16, name="first", offset=0, align_bytes=64)
         third = keep.tile([P, PACK, PIECE], BF16, name="third", tag="x_codes", align_bytes=64)
         fourth = keep.tile([P, PACK, PIECE], BF16, name="fourth", tag="w1_codes", align_bytes=64)
         for planes, e0, e1 in ((first, 0, 2 * PIECE), (third, 2 * PIECE, 3 * PIECE), (fourth, 3 * PIECE, 4 * PIECE)):
@@ -132,11 +150,12 @@ def tile_picked_winmax_relu_p_kernel(tc, x_words, x_scales, w1, w2, w3, offs, or
                 gather(planes, t, e0, e1)
         pairs = [first[:, :, :PIECE], first[:, :, PIECE:], third[:], fourth[:]]
 
-        w_codes = keep.tile([P, 2 * N], U32, name="w_codes", align_bytes=64)
-        w_plane = keep.tile([P, 2 * N], U8, name="w_plane", align_bytes=64)
-        nc.vector.quantize_mx(out=w_codes[:].bitcast(FP8X4), scales=w_plane[:], in_=w_bf[:])
+        w_codes = keep.tile([P, 3 * half], U32, name="w_codes", tag="picked", align_bytes=64)
+        w_plane = keep.tile([P, 3 * half], U8, name="w_plane", align_bytes=64)
+        for c0, c1 in ((0, N), (N, 3 * half)):
+            nc.vector.quantize_mx(out=w_codes[:, c0:c1].bitcast(FP8X4), scales=w_plane[:, c0:c1], in_=w_bf[:, PACK * c0 : PACK * c1])
 
-        z_bf = keep.tile([P, 2 * V * PACK], BF16, name="z_bf", tag="w_bf", align_bytes=64)
+        z_bf = shared.tile([P, 2 * V * PACK], BF16, name="z_bf", offset=4096, align_bytes=64)
         z_codes = keep.tile([P, 2 * V], U32, name="z_codes", align_bytes=64)
         z_plane = keep.tile([P, 2 * V], U8, name="z_plane", align_bytes=64)
         out_rows = out.rearrange("(m p) v -> p m v", p=P)
@@ -156,12 +175,13 @@ def tile_picked_winmax_relu_p_kernel(tc, x_words, x_scales, w1, w2, w3, offs, or
             nc.vector.quantize_mx(out=z_codes[:, c0:c1].bitcast(FP8X4), scales=z_plane[:, c0:c1], in_=z_bf[:, PACK * c0 : PACK * c1])
 
         def one_pass(res, c, u, m):
-            w_cols = slice(u * N + m * P, u * N + (m + 1) * P)
+            codes, plane, c0 = (early_codes, early_plane, 0) if u * N + m * P < half else (w_codes, w_plane, half)
+            w_cols = slice(u * N + m * P - c0, u * N + (m + 1) * P - c0)
             z_cols = slice((2 * c + u) * CHUNK, (2 * c + u + 1) * CHUNK)
             nc.tensor.matmul_mx(
                 out=res,
-                lhsT=w_codes[:, w_cols].bitcast(FP8X4),
-                lhsT_scale=w_plane[:, w_cols],
+                lhsT=codes[:, w_cols].bitcast(FP8X4),
+                lhsT_scale=plane[:, w_cols],
                 rhs=z_codes[:, z_cols].bitcast(FP8X4),
                 rhs_scale=z_plane[:, z_cols],
                 start=(u == 0),
@@ -192,11 +212,16 @@ def tile_picked_winmax_relu_p_kernel(tc, x_words, x_scales, w1, w2, w3, offs, or
 
         last = V // CHUNK - 1
         pool_pairs(0, 0)
-        for c in range(last):
+        for c in range(last - 1):
             pool_pairs(c, 1)
             pool_pairs(c + 1, 0)
             quantize_pooled(c, 0, 2)
             project(c)
+        pool_pairs(last - 1, 1)
+        quantize_pooled(last - 1, 0, 1)
+        quantize_pooled(last - 1, 1, 2)
+        project(last - 1)
+        pool_pairs(last, 0)
         pool_pairs(last, 1)
         quantize_pooled(last, 0, 1)
         quantize_pooled(last, 1, 2)

@@ -161,10 +161,10 @@ def tile_picked_winmax_relu_p_kernel(tc, x_words, x_scales, w1, w2, w3, offs, or
         out_rows = out.rearrange("(m p) v -> p m v", p=P)
 
         def pool_pairs(c, u):
-            members = pairs[c].rearrange("p t (g i s) -> p g t i s", i=2, s=2)
+            members = pairs[c].rearrange("p t (g i s) -> p g t i s", i=4, s=2)
             z0 = (2 * c + u) * CHUNK * PACK
             nc.vector.tensor_tensor(
-                z_bf[:, z0 : z0 + CHUNK * PACK].rearrange("p (g i t) -> p g t i", i=2, t=PACK),
+                z_bf[:, z0 : z0 + CHUNK * PACK].rearrange("p (g i t) -> p g t i", i=4, t=PACK),
                 members[:, :, :, :, 0],
                 members[:, :, :, :, 1],
                 (MAX, MIN)[u],

@@ -74,9 +74,9 @@ def tile_picked_winmax_relu_p_kernel(tc, x_words, x_scales, w1, w2, w3, offs, or
         w1_bf = keep.tile([P, PACK, P, PACK], BF16, name="w1_bf", align_bytes=64)
         for cast, h, m0, m1, t0, t1 in (
             (nc.scalar.copy, 0, 0, 64, 0, 4),
-            (nc.scalar.copy, 1, 0, 28, 0, 4),
-            (nc.vector.tensor_copy, 1, 28, 64, 0, 2),
-            (nc.vector.tensor_copy, 1, 28, 64, 2, 4),
+            (nc.scalar.copy, 1, 0, 22, 0, 4),
+            (nc.vector.tensor_copy, 1, 22, 64, 0, 2),
+            (nc.vector.tensor_copy, 1, 22, 64, 2, 4),
         ):
             cast(
                 w1_bf[:, t0:t1, h * (P // 2) + m0 : h * (P // 2) + m1, :].rearrange("p t m j -> p m j t"),
@@ -113,17 +113,15 @@ def tile_picked_winmax_relu_p_kernel(tc, x_words, x_scales, w1, w2, w3, offs, or
 
         early_codes = keep.tile([P, half], U32, name="early_codes", align_bytes=64)
         early_plane = keep.tile([P, half], U8, name="early_plane", align_bytes=64)
-        early_bf = shared.tile([P, PACK * half], BF16, name="early_bf", offset=3072, align_bytes=64)
+        early_bf = [shared.tile([P, PACK * P], BF16, name="early_bf%d" % m, offset=3072 + 1024 * m, align_bytes=64) for m in range(2)]
         for m in range(2):
             nc.vector.tensor_copy(
-                early_bf[:, m * PACK * P : (m + 1) * PACK * P].rearrange("p (c i j) -> p c j i", i=4, j=PACK),
+                early_bf[m][:].rearrange("p (c i j) -> p c j i", i=4, j=PACK),
                 raw_halves[0][:, :, m * P : (m + 1) * P].rearrange("p j (c i) -> p c j i", i=4),
             )
         for m in range(2):
             cols = slice(m * P, (m + 1) * P)
-            nc.vector.quantize_mx(
-                out=early_codes[:, cols].bitcast(FP8X4), scales=early_plane[:, cols], in_=early_bf[:, m * PACK * P : (m + 1) * PACK * P]
-            )
+            nc.vector.quantize_mx(out=early_codes[:, cols].bitcast(FP8X4), scales=early_plane[:, cols], in_=early_bf[m][:])
         w_bf = shared.tile([P, 3 * PACK * half], BF16, name="w_bf", offset=4096, align_bytes=64)
         for i in range(3):
             nc.gpsimd.tensor_scalar(
@@ -194,8 +192,10 @@ def tile_picked_winmax_relu_p_kernel(tc, x_words, x_scales, w1, w2, w3, offs, or
             for m in range(N // P):
                 for u in range(2):
                     one_pass(bank[:, m, :], c, u, m)
-            nc.scalar.copy(staged[:], bank[:])
-            nc.sync.dma_start(out_rows[:, :, c * CHUNK : (c + 1) * CHUNK], staged[:])
+            step = 2 if c == 0 else N // P
+            for m in range(0, N // P, step):
+                nc.scalar.copy(staged[:, m : m + step, :], bank[:, m : m + step, :])
+                nc.sync.dma_start(out_rows[:, m : m + step, c * CHUNK : (c + 1) * CHUNK], staged[:, m : m + step, :])
 
         def project_last(c):
             staged = keep.tile([P, N // P, CHUNK], F32, name="staged%d" % c, align_bytes=64)
@@ -219,9 +219,9 @@ def tile_picked_winmax_relu_p_kernel(tc, x_words, x_scales, w1, w2, w3, offs, or
             project(c)
         pool_pairs(last - 1, 1)
         quantize_pooled(last - 1, 0, 1)
+        pool_pairs(last, 0)
         quantize_pooled(last - 1, 1, 2)
         project(last - 1)
-        pool_pairs(last, 0)
         pool_pairs(last, 1)
         quantize_pooled(last, 0, 1)
         quantize_pooled(last, 1, 2)

@@ -30,6 +30,7 @@ def tile_picked_winmax_relu_p_kernel(tc, x_words, x_scales, w1, w2, w3, offs, or
     with ExitStack() as ctx:
         keep = ctx.enter_context(tc.tile_pool(name="keep", bufs=1))
         shared = ctx.enter_context(tc.tile_pool(name="shared", bufs=1))
+        stage = ctx.enter_context(tc.tile_pool(name="stage", bufs=1))
         psum = ctx.enter_context(tc.psum_pool(name="psum", bufs=1))
 
         offs_sb = keep.tile([P, S // 16], U16, name="offs_sb")
@@ -51,7 +52,7 @@ def tile_picked_winmax_relu_p_kernel(tc, x_words, x_scales, w1, w2, w3, offs, or
 
         x_plane = keep.tile([P, S], U8, name="x_plane", align_bytes=64)
         nc.vector.memset(x_plane[:].bitcast(I32), 0)
-        picked_scales = keep.tile([P, S], U8, name="picked_scales", tag="picked", align_bytes=64)
+        picked_scales = stage.tile([P, S], U8, name="picked_scales", offset=4608, align_bytes=64)
         nc.vector.tensor_copy(picked_scales[:], scale_table[:].indirect(offs_sb[:]))
         for q in range(4):
             nc.sync.dma_start(
@@ -59,14 +60,13 @@ def tile_picked_winmax_relu_p_kernel(tc, x_words, x_scales, w1, w2, w3, offs, or
                 picked_scales[32 * q : 32 * q + 32 : 8, :].bitcast(I32),
             )
         half = N // 2
-        raw_halves = []
-        for w, tag in ((w2, "late"), (w3, "picked")):
-            raw = keep.tile([P, PACK * N], F32, name="raw_" + tag, tag=tag, align_bytes=64)
-            rows = w.rearrange("(p j) c -> p j c", j=PACK)
-            for h in range(2):
-                view = raw[:, h * PACK * half : (h + 1) * PACK * half].rearrange("p (j c) -> p j c", j=PACK)
-                nc.sync.dma_start(view, rows[:, :, h * half : (h + 1) * half])
-                raw_halves.append(view)
+        w2_raw = keep.tile([P, PACK * N], F32, name="w2_raw", tag="late", align_bytes=64)
+        flat_halves = [w2_raw[:, h * PACK * half : (h + 1) * PACK * half] for h in range(2)]
+        flat_halves += [stage.tile([P, PACK * half], F32, name="w3_raw%d" % h, offset=1024 + 4096 * h, align_bytes=64)[:] for h in range(2)]
+        raw_halves = [flat.rearrange("p (j c) -> p j c", j=PACK) for flat in flat_halves]
+        for i, view in enumerate(raw_halves):
+            rows = (w2, w3)[i // 2].rearrange("(p j) c -> p j c", j=PACK)
+            nc.sync.dma_start(view, rows[:, :, i % 2 * half : (i % 2 + 1) * half])
 
         x_codes = keep.tile([P, S], U32, name="x_codes", tag="x_codes", align_bytes=64)
         nc.vector.tensor_copy(x_codes[:], word_table[:].indirect(offs_sb[:]))
@@ -92,7 +92,7 @@ def tile_picked_winmax_relu_p_kernel(tc, x_words, x_scales, w1, w2, w3, offs, or
                 scales=w1_plane[:, cols],
                 in_=w1_bf[:, t0:t1, :, :].rearrange("p t m j -> p (t m j)"),
             )
-        widths = [(256, 256, 256, 128, 128), (512, 512), (512, 512), (512, 512)]
+        widths = [(256, 256, 256, 128, 128), (512, 512), (512, 512), (512, 256, 256)]
         passes = [(t, sum(w[:i]), sum(w[: i + 1])) for t, w in enumerate(widths) for i in range(len(w))]
         for i, (t, s0, s1) in enumerate(passes):
             cols = slice(t * P, (t + 1) * P)
@@ -122,8 +122,8 @@ def tile_picked_winmax_relu_p_kernel(tc, x_words, x_scales, w1, w2, w3, offs, or
         for m in range(2):
             cols = slice(m * P, (m + 1) * P)
             nc.vector.quantize_mx(out=early_codes[:, cols].bitcast(FP8X4), scales=early_plane[:, cols], in_=early_bf[m][:])
-        w_bf = shared.tile([P, 3 * PACK * half], BF16, name="w_bf", offset=4096, align_bytes=64)
-        for i in range(3):
+        w_bf = shared.tile([P, 2 * PACK * half], BF16, name="w_bf", offset=4096, align_bytes=64)
+        for i in range(2):
             nc.gpsimd.tensor_scalar(
                 w_bf[:, i * PACK * half : (i + 1) * PACK * half].rearrange("p (c j) -> p c j", j=PACK),
                 raw_halves[i + 1].rearrange("p j c -> p c j"),
@@ -148,10 +148,23 @@ def tile_picked_winmax_relu_p_kernel(tc, x_words, x_scales, w1, w2, w3, offs, or
                 gather(planes, t, e0, e1)
         pairs = [first[:, :, :PIECE], first[:, :, PIECE:], third[:], fourth[:]]
 
-        w_codes = keep.tile([P, 3 * half], U32, name="w_codes", tag="picked", align_bytes=64)
+        late_bf = stage.tile([P, PACK * half], BF16, name="late_bf", offset=0, align_bytes=64)
+        nc.gpsimd.tensor_scalar(
+            late_bf[:, : PACK * P].rearrange("p (c j) -> p c j", j=PACK),
+            raw_halves[3][:, :, :P].rearrange("p j c -> p c j"),
+            1.0,
+            0.0,
+            MULT,
+            ADD,
+        )
+        nc.vector.tensor_copy(
+            late_bf[:, PACK * P :].rearrange("p (c i j) -> p c j i", i=4, j=PACK),
+            raw_halves[3][:, :, P:].rearrange("p j (c i) -> p c j i", i=4),
+        )
+        w_codes = stage.tile([P, 3 * half], U32, name="w_codes", offset=2048, align_bytes=64)
         w_plane = keep.tile([P, 3 * half], U8, name="w_plane", align_bytes=64)
-        for c0, c1 in ((0, N), (N, 3 * half)):
-            nc.vector.quantize_mx(out=w_codes[:, c0:c1].bitcast(FP8X4), scales=w_plane[:, c0:c1], in_=w_bf[:, PACK * c0 : PACK * c1])
+        for c0, c1, bf in ((0, N, w_bf), (N, 3 * half, late_bf)):
+            nc.vector.quantize_mx(out=w_codes[:, c0:c1].bitcast(FP8X4), scales=w_plane[:, c0:c1], in_=bf[:])
 
         z_bf = shared.tile([P, 2 * V * PACK], BF16, name="z_bf", offset=4096, align_bytes=64)
         z_codes = keep.tile([P, 2 * V], U32, name="z_codes", align_bytes=64)

@@ -113,7 +113,7 @@ def tile_picked_winmax_relu_p_kernel(tc, x_words, x_scales, w1, w2, w3, offs, or
 
         early_codes = keep.tile([P, half], U32, name="early_codes", align_bytes=64)
         early_plane = keep.tile([P, half], U8, name="early_plane", align_bytes=64)
-        early_bf = [shared.tile([P, PACK * P], BF16, name="early_bf%d" % m, offset=3072 + 1024 * m, align_bytes=64) for m in range(2)]
+        early_bf = [shared.tile([P, PACK * P], BF16, name="early_bf%d" % m, offset=4096 - 1024 * m, align_bytes=64) for m in range(2)]
         for m in range(2):
             nc.vector.tensor_copy(
                 early_bf[m][:].rearrange("p (c i j) -> p c j i", i=4, j=PACK),
@@ -125,8 +125,8 @@ def tile_picked_winmax_relu_p_kernel(tc, x_words, x_scales, w1, w2, w3, offs, or
         w_bf = shared.tile([P, 2 * PACK * half], BF16, name="w_bf", offset=4096, align_bytes=64)
         for i in range(2):
             nc.gpsimd.tensor_scalar(
-                w_bf[:, i * PACK * half : (i + 1) * PACK * half].rearrange("p (c j) -> p c j", j=PACK),
-                raw_halves[i + 1].rearrange("p j c -> p c j"),
+                w_bf[:, i * PACK * half : (i + 1) * PACK * half].rearrange("p (c i j) -> p c j i", i=4, j=PACK),
+                raw_halves[i + 1].rearrange("p j (c i) -> p c j i", i=4),
                 1.0,
                 0.0,
                 MULT,
@@ -150,16 +150,16 @@ def tile_picked_winmax_relu_p_kernel(tc, x_words, x_scales, w1, w2, w3, offs, or
 
         late_bf = stage.tile([P, PACK * half], BF16, name="late_bf", offset=0, align_bytes=64)
         nc.gpsimd.tensor_scalar(
-            late_bf[:, : PACK * P].rearrange("p (c j) -> p c j", j=PACK),
-            raw_halves[3][:, :, :P].rearrange("p j c -> p c j"),
+            late_bf[:, : PACK * 96].rearrange("p (c i j) -> p c j i", i=4, j=PACK),
+            raw_halves[3][:, :, :96].rearrange("p j (c i) -> p c j i", i=4),
             1.0,
             0.0,
             MULT,
             ADD,
         )
         nc.vector.tensor_copy(
-            late_bf[:, PACK * P :].rearrange("p (c i j) -> p c j i", i=4, j=PACK),
-            raw_halves[3][:, :, P:].rearrange("p j (c i) -> p c j i", i=4),
+            late_bf[:, PACK * 96 :].rearrange("p (c i j) -> p c j i", i=4, j=PACK),
+            raw_halves[3][:, :, 96:].rearrange("p j (c i) -> p c j i", i=4),
         )
         w_codes = stage.tile([P, 3 * half], U32, name="w_codes", offset=2048, align_bytes=64)
         w_plane = keep.tile([P, 3 * half], U8, name="w_plane", align_bytes=64)

from contextlib import ExitStack

import concourse.mybir as mybir

K, T, S, V, N, H = 512, 2048, 1024, 512, 512, 512
FLOPS = 2 * K * H * S + 2 * 2 * H * N * V

F32 = mybir.dt.float32
BF16 = mybir.dt.bfloat16
I32 = mybir.dt.int32
U32 = mybir.dt.uint32
U16 = mybir.dt.uint16
U8 = mybir.dt.uint8
FP8X4 = mybir.dt.float8_e4m3fn_x4
RELU = mybir.ActivationFunctionType.Relu
COPY = mybir.ActivationFunctionType.Copy
MAX = mybir.AluOpType.max
MIN = mybir.AluOpType.min
MULT = mybir.AluOpType.mult
ADD = mybir.AluOpType.add

P = 128
PACK = 4
CHUNK = 128
PIECE = 256


def tile_picked_winmax_relu_p_kernel(tc, x_words, x_scales, w1, w2, w3, offs, order, out):
    nc = tc.nc
    with ExitStack() as ctx:
        keep = ctx.enter_context(tc.tile_pool(name="keep", bufs=1))
        shared = ctx.enter_context(tc.tile_pool(name="shared", bufs=1))
        stage = ctx.enter_context(tc.tile_pool(name="stage", bufs=1))
        psum = ctx.enter_context(tc.psum_pool(name="psum", bufs=1))

        offs_sb = keep.tile([P, S // 16], U16, name="offs_sb")
        order_sb = keep.tile([P, S // 16], U16, name="order_sb")
        scale_table = keep.tile([P, T], U8, name="scale_table", tag="late", align_bytes=64)
        word_table = keep.tile([P, T], U32, name="word_table", align_bytes=64)
        w1_raw = [keep.tile([P, PACK, H // 2], F32, name="w1_raw%d" % h, align_bytes=64) for h in range(2)]

        nc.vector.memset(scale_table[:].bitcast(I32), 0)
        nc.sync.dma_start(offs_sb[:], offs)
        words = x_words[0].rearrange("p c r -> p (c r)").bitcast(I32)
        nc.sync.dma_start(word_table[:, :256].bitcast(I32), words[:, :256])
        nc.sync.dma_start(scale_table[0:P:8, :].bitcast(I32), x_scales[0].bitcast(I32))
        nc.sync.dma_start(word_table[:, 256:].bitcast(I32), words[:, 256:])
        w1_rows = w1.rearrange("(p j) c -> p j c", j=PACK)
        for h in range(2):
            nc.sync.dma_start(w1_raw[h][:], w1_rows[:, :, h * (H // 2) : (h + 1) * (H // 2)])
        nc.sync.dma_start(order_sb[:], order)

        x_plane = keep.tile([P, S], U8, name="x_plane", align_bytes=64)
        nc.vector.memset(x_plane[:].bitcast(I32), 0)
        picked_scales = stage.tile([P, S], U8, name="picked_scales", offset=4608, align_bytes=64)
        nc.vector.tensor_copy(picked_scales[:], scale_table[:].indirect(offs_sb[:]))
        for q in range(4):
            nc.sync.dma_start(
                x_plane[32 * q : 32 * q + 4, :].bitcast(I32),
                picked_scales[32 * q : 32 * q + 32 : 8, :].bitcast(I32),
            )
        half = N // 2
        w2_raw = keep.tile([P, PACK * N], F32, name="w2_raw", tag="late", align_bytes=64)
        flat_halves = [w2_raw[:, h * PACK * half : (h + 1) * PACK * half] for h in range(2)]
        flat_halves += [stage.tile([P, PACK * half], F32, name="w3_raw%d" % h, offset=1024 + 4096 * h, align_bytes=64)[:] for h in range(2)]
        raw_halves = [flat.rearrange("p (j c) -> p j c", j=PACK) for flat in flat_halves]
        for i, view in enumerate(raw_halves):
            rows = (w2, w3)[i // 2].rearrange("(p j) c -> p j c", j=PACK)
            nc.sync.dma_start(view, rows[:, :, i % 2 * half : (i % 2 + 1) * half])

        x_codes = keep.tile([P, S], U32, name="x_codes", tag="x_codes", align_bytes=64)
        nc.vector.tensor_copy(x_codes[:], word_table[:].indirect(offs_sb[:]))

        w1_bf = keep.tile([P, PACK, P, PACK], BF16, name="w1_bf", align_bytes=64)
        for cast, h, m0, m1, t0, t1 in (
            (nc.scalar.copy, 0, 0, 64, 0, 4),
            (nc.scalar.copy, 1, 0, 22, 0, 4),
            (nc.vector.tensor_copy, 1, 22, 64, 0, 2),
            (nc.vector.tensor_copy, 1, 22, 64, 2, 4),
        ):
            cast(
                w1_bf[:, t0:t1, h * (P // 2) + m0 : h * (P // 2) + m1, :].rearrange("p t m j -> p m j t"),
                w1_raw[h][:].rearrange("p j (m t) -> p m j t", t=PACK)[:, m0:m1, :, t0:t1],
            )
        w1_codes = keep.tile([P, H], U32, name="w1_codes", tag="w1_codes", align_bytes=64)
        w1_plane = keep.tile([P, H], U8, name="w1_plane", align_bytes=64)
        y = [keep.tile([P, S], F32, name="y%d" % t, align_bytes=64) for t in range(PACK)]
        for t0, t1 in ((0, 1), (1, 2), (2, 4)):
            cols = slice(t0 * P, t1 * P)
            nc.vector.quantize_mx(
                out=w1_codes[:, cols].bitcast(FP8X4),
                scales=w1_plane[:, cols],
                in_=w1_bf[:, t0:t1, :, :].rearrange("p t m j -> p (t m j)"),
            )
        widths = [(256, 256, 256, 128, 128), (512, 512), (512, 512), (512, 256, 256)]
        passes = [(t, sum(w[:i]), sum(w[: i + 1])) for t, w in enumerate(widths) for i in range(len(w))]
        for i, (t, s0, s1) in enumerate(passes):
            cols = slice(t * P, (t + 1) * P)
            acc = psum.tile([P, s1 - s0], F32, name="acc", tag="bank%d" % (i % 8))
            nc.tensor.matmul_mx(
                out=acc[:],
                lhsT=w1_codes[:, cols].bitcast(FP8X4),
                lhsT_scale=w1_plane[:, cols],
                rhs=x_codes[:, s0:s1].bitcast(FP8X4),
                rhs_scale=x_plane[:, s0:s1],
                start=True,
                stop=True,
            )
            if i == len(passes) - 1:
                nc.vector.tensor_scalar_max(y[t][:, s0:s1], acc[:], 0.0)
            else:
                nc.scalar.activation(y[t][:, s0:s1], acc[:], RELU)

        early_codes = keep.tile([P, half], U32, name="early_codes", align_bytes=64)
        early_plane = keep.tile([P, half], U8, name="early_plane", align_bytes=64)
        early_bf = [shared.tile([P, PACK * P], BF16, name="early_bf%d" % m, offset=4096 - 1024 * m, align_bytes=64) for m in range(2)]
        for m in range(2):
            nc.vector.tensor_copy(
                early_bf[m][:].rearrange("p (c i j) -> p c j i", i=4, j=PACK),
                raw_halves[0][:, :, m * P : (m + 1) * P].rearrange("p j (c i) -> p c j i", i=4),
            )
        for m in range(2):
            cols = slice(m * P, (m + 1) * P)
            nc.vector.quantize_mx(out=early_codes[:, cols].bitcast(FP8X4), scales=early_plane[:, cols], in_=early_bf[m][:])
        w_bf = shared.tile([P, 2 * PACK * half], BF16, name="w_bf", offset=4096, align_bytes=64)
        for i in range(2):
            nc.gpsimd.tensor_scalar(
                w_bf[:, i * PACK * half : (i + 1) * PACK * half].rearrange("p (c i j) -> p c j i", i=4, j=PACK),
                raw_halves[i + 1].rearrange("p j (c i) -> p c j i", i=4),
                1.0,
                0.0,
                MULT,
                ADD,
            )

        def gather(planes, t, e0, e1):
            looked_up = y[t][:].indirect(order_sb[:, e0 // 16 : e1 // 16])
            if e0 == 0 and t < PACK - 1:
                nc.vector.tensor_copy(planes[:, t, :], looked_up)
            else:
                nc.scalar.activation(planes[:, t, :], looked_up, COPY)

        first = shared.tile([P, PACK, 2 * PIECE], BF16, name="first", offset=0, align_bytes=64)
        third = keep.tile([P, PACK, PIECE], BF16, name="third", tag="x_codes", align_bytes=64)
        fourth = keep.tile([P, PACK, PIECE], BF16, name="fourth", tag="w1_codes", align_bytes=64)
        for planes, e0, e1 in ((first, 0, 2 * PIECE), (third, 2 * PIECE, 3 * PIECE), (fourth, 3 * PIECE, 4 * PIECE)):
            for t in range(PACK):
                gather(planes, t, e0, e1)
        pairs = [first[:, :, :PIECE], first[:, :, PIECE:], third[:], fourth[:]]

        late_bf = stage.tile([P, PACK * half], BF16, name="late_bf", offset=0, align_bytes=64)
        nc.gpsimd.tensor_scalar(
            late_bf[:, : PACK * 96].rearrange("p (c i j) -> p c j i", i=4, j=PACK),
            raw_halves[3][:, :, :96].rearrange("p j (c i) -> p c j i", i=4),
            1.0,
            0.0,
            MULT,
            ADD,
        )
        nc.vector.tensor_copy(
            late_bf[:, PACK * 96 :].rearrange("p (c i j) -> p c j i", i=4, j=PACK),
            raw_halves[3][:, :, 96:].rearrange("p j (c i) -> p c j i", i=4),
        )
        w_codes = stage.tile([P, 3 * half], U32, name="w_codes", offset=2048, align_bytes=64)
        w_plane = keep.tile([P, 3 * half], U8, name="w_plane", align_bytes=64)
        for c0, c1, bf in ((0, N, w_bf), (N, 3 * half, late_bf)):
            nc.vector.quantize_mx(out=w_codes[:, c0:c1].bitcast(FP8X4), scales=w_plane[:, c0:c1], in_=bf[:])

        z_bf = shared.tile([P, 2 * V * PACK], BF16, name="z_bf", offset=4096, align_bytes=64)
        z_codes = keep.tile([P, 2 * V], U32, name="z_codes", align_bytes=64)
        z_plane = keep.tile([P, 2 * V], U8, name="z_plane", align_bytes=64)
        out_rows = out.rearrange("(m p) v -> p m v", p=P)

        def pool_pairs(c, u):
            members = pairs[c].rearrange("p t (g i s) -> p g t i s", i=4, s=2)
            z0 = (2 * c + u) * CHUNK * PACK
            nc.vector.tensor_tensor(
                z_bf[:, z0 : z0 + CHUNK * PACK].rearrange("p (g i t) -> p g t i", i=4, t=PACK),
                members[:, :, :, :, 0],
                members[:, :, :, :, 1],
                (MAX, MIN)[u],
            )

        def quantize_pooled(c, u0, u1):
            c0, c1 = (2 * c + u0) * CHUNK, (2 * c + u1) * CHUNK
            nc.vector.quantize_mx(out=z_codes[:, c0:c1].bitcast(FP8X4), scales=z_plane[:, c0:c1], in_=z_bf[:, PACK * c0 : PACK * c1])

        def one_pass(res, c, u, m):
            codes, plane, c0 = (early_codes, early_plane, 0) if u * N + m * P < half else (w_codes, w_plane, half)
            w_cols = slice(u * N + m * P - c0, u * N + (m + 1) * P - c0)
            z_cols = slice((2 * c + u) * CHUNK, (2 * c + u + 1) * CHUNK)
            nc.tensor.matmul_mx(
                out=res,
                lhsT=codes[:, w_cols].bitcast(FP8X4),
                lhsT_scale=plane[:, w_cols],
                rhs=z_codes[:, z_cols].bitcast(FP8X4),
                rhs_scale=z_plane[:, z_cols],
                start=(u == 0),
                stop=(u == 1),
            )

        def project(c):
            staged = keep.tile([P, N // P, CHUNK], F32, name="staged%d" % c, align_bytes=64)
            bank = psum.tile([P, N // P, CHUNK], F32, name="res", tag="bank%d" % c)
            for m in range(N // P):
                for u in range(2):
                    one_pass(bank[:, m, :], c, u, m)
            step = 2 if c == 0 else N // P
            for m in range(0, N // P, step):
                nc.scalar.copy(staged[:, m : m + step, :], bank[:, m : m + step, :])
                nc.sync.dma_start(out_rows[:, m : m + step, c * CHUNK : (c + 1) * CHUNK], staged[:, m : m + step, :])

        def project_last(c):
            staged = keep.tile([P, N // P, CHUNK], F32, name="staged%d" % c, align_bytes=64)
            banks = [psum.tile([P, CHUNK], F32, name="res", tag="bank%d" % (4 + m)) for m in range(N // P)]
            for u in range(2):
                for m in range(N // P):
                    one_pass(banks[m][:], c, u, m)
            for m in range(N // P):
                by_vector = m % 2 == 1
                (nc.vector.tensor_copy if by_vector else nc.scalar.copy)(staged[:, m, :], banks[m][:])
                (nc.sync if by_vector else nc.scalar).dma_start(
                    out_rows[:, m : m + 1, c * CHUNK : (c + 1) * CHUNK], staged[:, m : m + 1, :]
                )

        last = V // CHUNK - 1
        pool_pairs(0, 0)
        for c in range(last - 1):
            pool_pairs(c, 1)
            pool_pairs(c + 1, 0)
            quantize_pooled(c, 0, 2)
            project(c)
        pool_pairs(last - 1, 1)
        quantize_pooled(last - 1, 0, 1)
        pool_pairs(last, 0)
        quantize_pooled(last - 1, 1, 2)
        project(last - 1)
        pool_pairs(last, 1)
        quantize_pooled(last, 0, 1)
        quantize_pooled(last, 1, 2)
        project_last(last)
